import numpy as np
import ml_dtypes


def mxq(x, axis, fmt="e4m3"):
    dtype, down = {"e4m3": (ml_dtypes.float8_e4m3fn, 7), "e5m2": (ml_dtypes.float8_e5m2, 14)}[fmt]
    v = np.moveaxis(np.asarray(x, np.float32).astype(ml_dtypes.bfloat16).astype(np.float64), axis, -1)
    blocks = v.reshape(v.shape[:-1] + (-1, 32))
    amax = np.abs(blocks).max(-1, keepdims=True)
    byte = np.maximum(np.where(amax > 0, np.frexp(amax)[1] - 1 + 127, 0) - down, 1)
    scale = np.exp2(byte - 127.0)
    codes = (blocks / scale).astype(np.float32).astype(dtype).astype(np.float64)
    return np.moveaxis((codes * scale).reshape(v.shape), -1, axis)


WIDE = False


def mx_kscale(k):
    if not WIDE:
        return np.ones(k)
    levels = np.array([30, -30])
    if k % 512:
        return np.exp2(np.random.permutation(np.resize(levels, k // 32))).repeat(32)
    a = np.empty((k // 512, 16))
    for p in range(k // 512):
        a[p, :8] = np.random.permutation(np.resize(levels, 8))
        for g in range(8):
            far = levels[np.abs(levels - a[p, g]) >= 10]
            a[p, g + 8] = far[np.random.randint(len(far))]
    return np.exp2(a.ravel()).repeat(32)


def f64(x):
    return np.asarray(x).astype(np.float64)


E2M1 = np.array([0.0, 0.5, 1.0, 1.5, 2.0, 3.0, 4.0, 6.0, -0.0, -0.5, -1.0, -1.5, -2.0, -3.0, -4.0, -6.0])


def pack_weight(w, fmt):
    k, n = w.shape
    w = f64(np.asarray(w, np.float32).astype(ml_dtypes.bfloat16)).reshape(k // 32, 32, n)
    amax = np.abs(w).max(1)
    if fmt == "e4m3":
        byte = np.frexp(amax)[1] - 1 + 127 - 7
    else:
        mant, ex = np.frexp(amax / 6.0)
        byte = np.where(mant > 0.5, ex, ex - 1) + 127
    byte = np.clip(np.where(amax > 0, byte, 1), 1, 254)
    scaled = (w * np.exp2(127.0 - byte)[:, None, :]).reshape(k, n).astype(np.float32)
    by_word = np.ascontiguousarray(scaled.reshape(k // 512, 128, 4, n).transpose(0, 1, 3, 2))
    if fmt == "e4m3":
        words = by_word.astype(ml_dtypes.float8_e4m3fn).view(np.uint8)
    else:
        c = by_word.astype(ml_dtypes.float4_e2m1fn).view(np.uint8) & 0xF
        words = (c[..., 0::2] | (c[..., 1::2] << 4)).reshape(k // 512, 128, 2 * n)
    return np.ascontiguousarray(words), np.ascontiguousarray(byte.astype(np.uint8).reshape(k // 512, 16, n))


def unpack_weight(words, scales, fmt):
    g, _, n = scales.shape
    words = np.ascontiguousarray(words).reshape(g, 128, n, -1)
    if fmt == "e4m3":
        vals = words.view(ml_dtypes.float8_e4m3fn).astype(np.float64)
    else:
        nib = np.empty((g, 128, n, 4), np.uint8)
        nib[..., 0::2] = words & 0xF
        nib[..., 1::2] = words >> 4
        vals = E2M1[nib]
    vals = vals * np.repeat(np.exp2(scales.astype(np.float64) - 127.0), 8, axis=1)[..., None]
    return vals.transpose(0, 1, 3, 2).reshape(g * 512, n)


def silu(v):
    return v / (1.0 + np.exp(-np.maximum(v, -700.0)))


K, L, R, M, T = 1024, 1024, 1024, 1024, 512


def setup_inputs():
    n = np.random.standard_normal
    s1 = mx_kscale(K)[:, None]
    s2 = mx_kscale(L)[:, None]
    u = mx_kscale(R)[:, None]
    p_w = pack_weight(n((R, M)) / np.sqrt(R) / u, "e2m1")
    return {
        "x": (n((K, T)) * s1).astype(np.float32),
        "wx": (n((K, R)) / np.sqrt(K) / s1 * u.T).astype(np.float32),
        "c": (n((L, T)) * s2).astype(np.float32),
        "wc": (n((L, R)) / np.sqrt(L) / s2).astype(np.float32),
        "w_words": p_w[0],
        "w_scales": p_w[1],
        "b": (0.3 * n(1024)).astype(np.float32),
    }


def reference(x, wx, c, wc, w_words, w_scales, b):
    x_ = mxq(f64(x), 0, "e4m3")
    wx_ = mxq(f64(wx), 0, "e4m3")
    c_ = mxq(f64(c), 0, "e5m2")
    wc_ = mxq(f64(wc), 0, "e4m3")
    w_ = unpack_weight(w_words, w_scales, "e2m1")
    h_ = mxq((wx_.T @ x_) * (wc_.T @ c_), 0, "e4m3")
    y = w_.T @ h_
    return silu(y + f64(b)[:, None])

@@ -1,0 +1,315 @@
+from contextlib import ExitStack
+
+import concourse.mybir as mybir
+from concourse.masks import make_identity
+
+K, R, M, T = 1024, 1024, 1024, 512
+FLOPS = 2 * (K * R * T + K * R * T + R * M * T)
+
+F32 = mybir.dt.float32
+BF16 = mybir.dt.bfloat16
+U32 = mybir.dt.uint32
+I32 = mybir.dt.int32
+U8 = mybir.dt.uint8
+E4M3 = mybir.dt.float8_e4m3fn_x4
+E5M2 = mybir.dt.float8_e5m2_x4
+E2M1 = mybir.dt.float4_e2m1fn_x4
+
+P = 128
+PACK = 4
+PASS = P * PACK
+CH = 128
+CHUNKS = T // CH
+
+
+def tile_mix_bilin_fm_silu_kernel(tc, x, wx, c, wc, w_words, w_scales, b, out):
+    nc = tc.nc
+    with ExitStack() as ctx:
+        keep = ctx.enter_context(tc.tile_pool(name="keep", bufs=1))
+        stage = ctx.enter_context(tc.tile_pool(name="stage", bufs=4))
+        psum = ctx.enter_context(tc.psum_pool(name="psum", bufs=1))
+        ctx.enter_context(tc.manual_schedule())
+
+        def bank(i):
+            return psum.tile([P, PASS], F32, name="bank%d" % i)
+
+        b_rows = keep.tile([P, P], F32, name="b_rows")
+        ident = keep.tile([P, P], F32, name="ident")
+        w_plane = keep.tile([P, 2, M], U8, name="w_plane", align_bytes=64)
+        nc.gpsimd.memset(b_rows[:], 0.0)
+        nc.gpsimd.memset(w_plane[:].rearrange("p a n -> p (a n)").bitcast(I32), 0)
+        make_identity(nc, ident[:])
+        nc.scalar.dma_start(out=b_rows[0 : M // P, :], in_=b.rearrange("(i p) -> i p", p=P))
+
+        raw = {}
+
+        def load(name, rows):
+            t = keep.tile([P, PACK, PASS], F32, name="raw_" + name)
+            nc.sync.dma_start(out=t[:], in_=rows.rearrange("(p i) w -> p i w", i=PACK))
+            raw[name] = t
+
+        def rows_of(g):
+            return slice(g * PASS, (g + 1) * PASS)
+
+        load("c0", c[rows_of(0), :])
+        load("wc00", wc[rows_of(0), rows_of(0)])
+        load("c1", c[rows_of(1), :])
+        load("wc10", wc[rows_of(1), rows_of(0)])
+        load("x0", x[rows_of(0), :])
+        load("wx00", wx[rows_of(0), rows_of(0)])
+        load("x1", x[rows_of(1), :])
+        load("wx10", wx[rows_of(1), rows_of(0)])
+        load("wc01", wc[rows_of(0), rows_of(1)])
+        load("wx01", wx[rows_of(0), rows_of(1)])
+        load("wc11", wc[rows_of(1), rows_of(1)])
+        load("wx11", wx[rows_of(1), rows_of(1)])
+        w_sc = w_scales.bitcast(I32)
+        for q in range(4):
+            nc.sync.dma_start(
+                out=w_plane[32 * q : 32 * q + 4, :, :].bitcast(I32),
+                in_=w_sc[:, 4 * q : 4 * q + 4, :].rearrange("a q n -> q a n"),
+            )
+        w_codes = []
+        for a in range(2):
+            t = keep.tile([P, 2 * M], U8, name="w_codes%d" % a, align_bytes=64)
+            nc.sync.dma_start(out=t[:].bitcast(I32), in_=w_words[a].bitcast(I32))
+            w_codes.append(t)
+
+        bias = keep.tile([P, M // P], F32, name="bias")
+
+        grouped = {}
+        codes = {}
+        scales = {}
+
+        def interleave(name, cols_v):
+            src = raw[name]
+            g = stage.tile([P, PASS * PACK], BF16, name="grouped", align_bytes=64)
+            grouped[name] = g
+            if name[0] == "w":
+                s = src[:].rearrange("p i (m j) -> p m i j", j=PACK)
+                d = g[:].rearrange("p (j m i) -> p m i j", j=PACK, i=PACK)
+            else:
+                s = src[:].rearrange("p i (m j) -> p m i j", j=PACK)
+                d = g[:].rearrange("p (m j i) -> p m i j", j=PACK, i=PACK)
+            mv = cols_v // PACK
+            if mv > 0:
+                nc.vector.tensor_copy(out=d[:, 0:mv], in_=s[:, 0:mv])
+            if mv < P:
+                nc.scalar.copy(out=d[:, mv:P], in_=s[:, mv:P])
+
+        def quantize(name, src, width, fmt):
+            cd = keep.tile([P, width], U32, name="codes_" + name, align_bytes=64)
+            sc = keep.tile([P, width], U8, name="scales_" + name, align_bytes=64)
+            nc.vector.quantize_mx(out=cd[:].bitcast(fmt), scales=sc[:], in_=src)
+            codes[name] = cd
+            scales[name] = sc
+
+        def quant_in(name):
+            quantize(name, grouped[name][:], PASS, E5M2 if name[0] == "c" else E4M3)
+
+        pc_bank = {}
+        pc = {}
+
+        def pc_pass(g, a):
+            wname = "wc%d%d" % (g, a)
+            cname = "c%d" % g
+            for j in range(PACK):
+                if g == 0:
+                    pc_bank[j] = bank(j)
+                cols = slice(j * P, (j + 1) * P)
+                nc.tensor.matmul_mx(
+                    out=pc_bank[j][:],
+                    lhsT=codes[wname][:, cols].bitcast(E4M3),
+                    lhsT_scale=scales[wname][:, cols],
+                    rhs=codes[cname][:].bitcast(E5M2),
+                    rhs_scale=scales[cname][:],
+                    start=(g == 0),
+                    stop=(g == 1),
+                )
+
+        def pc_copy_half(a, half):
+            pc[a, half] = keep.tile([P, PACK, 2 * CH], F32, name="pc%d%d" % (a, half))
+            for j in range(PACK):
+                nc.scalar.copy(out=pc[a, half][:, j, :], in_=pc_bank[j][:, half * 2 * CH : (half + 1) * 2 * CH])
+
+        def pc_copy(a):
+            whole = keep.tile([P, PACK, T], F32, name="pc%d" % a)
+            for j in range(PACK):
+                nc.scalar.copy(out=whole[:, j, :], in_=pc_bank[j][:])
+            for half in range(2):
+                pc[a, half] = whole[:, :, half * 2 * CH : (half + 1) * 2 * CH]
+
+        px_bank = {}
+
+        def px_pass(g, a, ch):
+            wname = "wx%d%d" % (g, a)
+            xname = "x%d" % g
+            if g == 0:
+                px_bank[ch] = bank(4 + ch)
+            tcols = slice(ch * CH, (ch + 1) * CH)
+            for j in range(PACK):
+                cols = slice(j * P, (j + 1) * P)
+                nc.tensor.matmul_mx(
+                    out=px_bank[ch][:, j * CH : (j + 1) * CH],
+                    lhsT=codes[wname][:, cols].bitcast(E4M3),
+                    lhsT_scale=scales[wname][:, cols],
+                    rhs=codes[xname][:, tcols].bitcast(E4M3),
+                    rhs_scale=scales[xname][:, tcols],
+                    start=(g == 0 and j == 0),
+                    stop=(g == 1 and j == PACK - 1),
+                )
+
+        h0 = keep.tile([P, T * PACK], BF16, name="h0", align_bytes=64)
+        h = {}
+        h_codes = [keep.tile([P, T], U32, name="h_codes%d" % a, align_bytes=64) for a in range(2)]
+        h_scales = [keep.tile([P, T], U8, name="h_scales%d" % a, align_bytes=64) for a in range(2)]
+
+        def mult(a, ch):
+            if a == 0:
+                h[a, ch] = h0[:, ch * CH * PACK : (ch + 1) * CH * PACK]
+            else:
+                t = keep.tile([P, CH * PACK], BF16, name="h1%d" % ch, align_bytes=64)
+                h[a, ch] = t[:]
+            nc.vector.tensor_tensor(
+                out=h[a, ch].rearrange("p (m i j) -> p m j i", i=PACK, j=PACK),
+                in0=px_bank[ch][:].rearrange("p (j m i) -> p m j i", j=PACK, i=PACK),
+                in1=pc[a, ch // 2][:, :, (ch % 2) * CH : (ch % 2 + 1) * CH].rearrange("p j (m i) -> p m j i", i=PACK),
+                op=mybir.AluOpType.mult,
+            )
+
+        def quant_h(a, ch):
+            cols = slice(ch * CH, (ch + 1) * CH)
+            nc.vector.quantize_mx(out=h_codes[a][:, cols].bitcast(E4M3), scales=h_scales[a][:, cols], in_=h[a, ch])
+
+        def quant_h_all(a):
+            nc.vector.quantize_mx(out=h_codes[a][:].bitcast(E4M3), scales=h_scales[a][:], in_=h0[:])
+
+        y_bank = {}
+
+        def y_mm(dst, a, nt, cols, start, stop):
+            nc.tensor.matmul_mx(
+                out=dst,
+                lhsT=w_codes[a][:, 2 * nt * P : 2 * (nt + 1) * P].bitcast(E2M1),
+                lhsT_scale=w_plane[:, a, nt * P : (nt + 1) * P],
+                rhs=h_codes[a][:, cols].bitcast(E4M3),
+                rhs_scale=h_scales[a][:, cols],
+                start=start,
+                stop=stop,
+            )
+
+        def y_half(a, half, pair):
+            if a == 0:
+                y_bank[half, pair] = bank(3 * half + pair)
+            for n2 in range(2):
+                for c2 in range(2):
+                    ch = 2 * half + c2
+                    col = (2 * n2 + c2) * CH
+                    y_mm(
+                        y_bank[half, pair][:, col : col + CH],
+                        a,
+                        2 * pair + n2,
+                        slice(ch * CH, (ch + 1) * CH),
+                        a == 0 and n2 == 0 and c2 == 0,
+                        a == 1 and n2 == 1 and c2 == 1,
+                    )
+
+        def y_full(a, nt):
+            if a == 0:
+                y_bank[nt] = bank(nt)
+            y_mm(y_bank[nt][:], a, nt, slice(0, T), a == 0, a == 1)
+
+        def finish_half(half, pair):
+            res = keep.tile([P, 2, 2 * CH], F32, name="res%d%d" % (half, pair))
+            for n2 in range(2):
+                nt = 2 * pair + n2
+                nc.scalar.activation(
+                    out=res[:, n2, :],
+                    in_=y_bank[half, pair][:, n2 * 2 * CH : (n2 + 1) * 2 * CH],
+                    func=mybir.ActivationFunctionType.Silu,
+                    bias=bias[:, nt : nt + 1],
+                )
+            nc.sync.dma_start(
+                out=out[2 * pair * P : 2 * (pair + 1) * P, half * 2 * CH : (half + 1) * 2 * CH].rearrange("(n p) t -> p n t", p=P),
+                in_=res[:],
+            )
+
+        def finish_full(nt):
+            res = keep.tile([P, T], F32, name="res%d" % nt)
+            nc.scalar.activation(
+                out=res[:], in_=y_bank[nt][:], func=mybir.ActivationFunctionType.Silu, bias=bias[:, nt : nt + 1]
+            )
+            nc.sync.dma_start(out=out[nt * P : (nt + 1) * P, :], in_=res[:])
+
+        def place_bias():
+            b_t = bank(4)
+            nc.tensor.transpose(b_t[:, 0:P], b_rows[:], ident[:])
+            nc.vector.tensor_copy(out=bias[:], in_=b_t[:, 0 : M // P])
+
+        interleave("c0", 320)
+        quant_in("c0")
+        interleave("wc00", 320)
+        quant_in("wc00")
+        pc_pass(0, 0)
+        interleave("c1", 320)
+        quant_in("c1")
+        place_bias()
+        interleave("wc10", 320)
+        quant_in("wc10")
+        pc_pass(1, 0)
+        interleave("x0", 512)
+        pc_copy(0)
+        quant_in("x0")
+        interleave("wx00", 384)
+        quant_in("wx00")
+        for ch in range(CHUNKS):
+            px_pass(0, 0, ch)
+        interleave("x1", 320)
+        quant_in("x1")
+        interleave("wx10", 320)
+        quant_in("wx10")
+        for ch in range(CHUNKS):
+            px_pass(1, 0, ch)
+        mult(0, 0)
+        interleave("wc01", 64)
+        mult(0, 1)
+        mult(0, 2)
+        mult(0, 3)
+        quant_in("wc01")
+        pc_pass(0, 1)
+        interleave("wx01", 192)
+        quant_h_all(0)
+        quant_in("wx01")
+        for ch in range(CHUNKS):
+            px_pass(0, 1, ch)
+        interleave("wc11", 320)
+        quant_in("wc11")
+        pc_pass(1, 1)
+        interleave("wx11", 320)
+        pc_copy_half(1, 0)
+        pc_copy_half(1, 1)
+        quant_in("wx11")
+        for ch in range(CHUNKS):
+            px_pass(1, 1, ch)
+        y_half(0, 0, 0)
+        y_half(0, 0, 1)
+        y_half(0, 0, 2)
+        mult(1, 0)
+        mult(1, 1)
+        quant_h(1, 0)
+        quant_h(1, 1)
+        mult(1, 2)
+        mult(1, 3)
+        quant_h(1, 2)
+        quant_h(1, 3)
+        for pair in range(3):
+            y_half(1, 0, pair)
+            finish_half(0, pair)
+        for pair in range(3):
+            y_half(0, 1, pair)
+        for pair in range(3):
+            y_half(1, 1, pair)
+            finish_half(1, pair)
+        for nt in range(6, 8):
+            y_full(0, nt)
+            y_full(1, nt)
+            finish_full(nt)

@@ -26,7 +26,7 @@ def tile_mix_bilin_fm_silu_kernel(tc, x, wx, c, wc, w_words, w_scales, b, out):
     nc = tc.nc
     with ExitStack() as ctx:
         keep = ctx.enter_context(tc.tile_pool(name="keep", bufs=1))
-        stage = ctx.enter_context(tc.tile_pool(name="stage", bufs=4))
+        stage = ctx.enter_context(tc.tile_pool(name="stage", bufs=6))
         psum = ctx.enter_context(tc.psum_pool(name="psum", bufs=1))
         ctx.enter_context(tc.manual_schedule())
 
@@ -46,22 +46,25 @@ def tile_mix_bilin_fm_silu_kernel(tc, x, wx, c, wc, w_words, w_scales, b, out):
         def load(name, rows):
             t = keep.tile([P, PACK, PASS], F32, name="raw_" + name)
             nc.sync.dma_start(out=t[:], in_=rows.rearrange("(p i) w -> p i w", i=PACK))
-            raw[name] = t
+            raw[name] = t[:]
 
         def rows_of(g):
             return slice(g * PASS, (g + 1) * PASS)
 
+        def load_whole(name, rows):
+            t = keep.tile([P, PACK, R], F32, name="raw_" + name)
+            nc.sync.dma_start(out=t[:], in_=rows.rearrange("(p i) w -> p i w", i=PACK))
+            for a in range(2):
+                raw[name + str(a)] = t[:, :, rows_of(a)]
+
         load("c0", c[rows_of(0), :])
-        load("wc00", wc[rows_of(0), rows_of(0)])
+        load_whole("wc0", wc[rows_of(0), :])
+        load_whole("wc1", wc[rows_of(1), :])
         load("c1", c[rows_of(1), :])
-        load("wc10", wc[rows_of(1), rows_of(0)])
         load("x0", x[rows_of(0), :])
-        load("wx00", wx[rows_of(0), rows_of(0)])
+        load_whole("wx0", wx[rows_of(0), :])
         load("x1", x[rows_of(1), :])
         load("wx10", wx[rows_of(1), rows_of(0)])
-        load("wc01", wc[rows_of(0), rows_of(1)])
-        load("wx01", wx[rows_of(0), rows_of(1)])
-        load("wc11", wc[rows_of(1), rows_of(1)])
         load("wx11", wx[rows_of(1), rows_of(1)])
         w_sc = w_scales.bitcast(I32)
         for q in range(4):
@@ -86,10 +89,10 @@ def tile_mix_bilin_fm_silu_kernel(tc, x, wx, c, wc, w_words, w_scales, b, out):
             g = stage.tile([P, PASS * PACK], BF16, name="grouped", align_bytes=64)
             grouped[name] = g
             if name[0] == "w":
-                s = src[:].rearrange("p i (m j) -> p m i j", j=PACK)
+                s = src.rearrange("p i (m j) -> p m i j", j=PACK)
                 d = g[:].rearrange("p (j m i) -> p m i j", j=PACK, i=PACK)
             else:
-                s = src[:].rearrange("p i (m j) -> p m i j", j=PACK)
+                s = src.rearrange("p i (m j) -> p m i j", j=PACK)
                 d = g[:].rearrange("p (m j i) -> p m i j", j=PACK, i=PACK)
             mv = cols_v // PACK
             if mv > 0:
@@ -115,10 +118,10 @@ def tile_mix_bilin_fm_silu_kernel(tc, x, wx, c, wc, w_words, w_scales, b, out):
             cname = "c%d" % g
             for j in range(PACK):
                 if g == 0:
-                    pc_bank[j] = bank(j)
+                    pc_bank[a, j] = bank(PACK * a + j)
                 cols = slice(j * P, (j + 1) * P)
                 nc.tensor.matmul_mx(
-                    out=pc_bank[j][:],
+                    out=pc_bank[a, j][:],
                     lhsT=codes[wname][:, cols].bitcast(E4M3),
                     lhsT_scale=scales[wname][:, cols],
                     rhs=codes[cname][:].bitcast(E5M2),
@@ -127,15 +130,13 @@ def tile_mix_bilin_fm_silu_kernel(tc, x, wx, c, wc, w_words, w_scales, b, out):
                     stop=(g == 1),
                 )
 
-        def pc_copy_half(a, half):
-            pc[a, half] = keep.tile([P, PACK, 2 * CH], F32, name="pc%d%d" % (a, half))
-            for j in range(PACK):
-                nc.scalar.copy(out=pc[a, half][:, j, :], in_=pc_bank[j][:, half * 2 * CH : (half + 1) * 2 * CH])
-
-        def pc_copy(a):
+        def pc_copy(a, on_vector):
             whole = keep.tile([P, PACK, T], F32, name="pc%d" % a)
             for j in range(PACK):
-                nc.scalar.copy(out=whole[:, j, :], in_=pc_bank[j][:])
+                if j < on_vector:
+                    nc.vector.tensor_copy(out=whole[:, j, :], in_=pc_bank[a, j][:])
+                else:
+                    nc.scalar.copy(out=whole[:, j, :], in_=pc_bank[a, j][:])
             for half in range(2):
                 pc[a, half] = whole[:, :, half * 2 * CH : (half + 1) * 2 * CH]
 
@@ -145,12 +146,12 @@ def tile_mix_bilin_fm_silu_kernel(tc, x, wx, c, wc, w_words, w_scales, b, out):
             wname = "wx%d%d" % (g, a)
             xname = "x%d" % g
             if g == 0:
-                px_bank[ch] = bank(4 + ch)
+                px_bank[a, ch] = bank(CHUNKS * a + ch)
             tcols = slice(ch * CH, (ch + 1) * CH)
             for j in range(PACK):
                 cols = slice(j * P, (j + 1) * P)
                 nc.tensor.matmul_mx(
-                    out=px_bank[ch][:, j * CH : (j + 1) * CH],
+                    out=px_bank[a, ch][:, j * CH : (j + 1) * CH],
                     lhsT=codes[wname][:, cols].bitcast(E4M3),
                     lhsT_scale=scales[wname][:, cols],
                     rhs=codes[xname][:, tcols].bitcast(E4M3),
@@ -159,20 +160,22 @@ def tile_mix_bilin_fm_silu_kernel(tc, x, wx, c, wc, w_words, w_scales, b, out):
                     stop=(g == 1 and j == PACK - 1),
                 )
 
-        h0 = keep.tile([P, T * PACK], BF16, name="h0", align_bytes=64)
         h = {}
+        h_half = {}
         h_codes = [keep.tile([P, T], U32, name="h_codes%d" % a, align_bytes=64) for a in range(2)]
         h_scales = [keep.tile([P, T], U8, name="h_scales%d" % a, align_bytes=64) for a in range(2)]
 
         def mult(a, ch):
-            if a == 0:
-                h[a, ch] = h0[:, ch * CH * PACK : (ch + 1) * CH * PACK]
-            else:
-                t = keep.tile([P, CH * PACK], BF16, name="h1%d" % ch, align_bytes=64)
+            if a == 1 or ch < 2:
+                t = keep.tile([P, CH * PACK], BF16, name="hc%d%d" % (a, ch), align_bytes=64)
                 h[a, ch] = t[:]
+            else:
+                if ch % 2 == 0:
+                    h_half[a, ch // 2] = keep.tile([P, 2 * CH * PACK], BF16, name="h0%d" % (ch // 2), align_bytes=64)
+                h[a, ch] = h_half[a, ch // 2][:, (ch % 2) * CH * PACK : (ch % 2 + 1) * CH * PACK]
             nc.vector.tensor_tensor(
                 out=h[a, ch].rearrange("p (m i j) -> p m j i", i=PACK, j=PACK),
-                in0=px_bank[ch][:].rearrange("p (j m i) -> p m j i", j=PACK, i=PACK),
+                in0=px_bank[a, ch][:].rearrange("p (j m i) -> p m j i", j=PACK, i=PACK),
                 in1=pc[a, ch // 2][:, :, (ch % 2) * CH : (ch % 2 + 1) * CH].rearrange("p j (m i) -> p m j i", i=PACK),
                 op=mybir.AluOpType.mult,
             )
@@ -181,8 +184,9 @@ def tile_mix_bilin_fm_silu_kernel(tc, x, wx, c, wc, w_words, w_scales, b, out):
             cols = slice(ch * CH, (ch + 1) * CH)
             nc.vector.quantize_mx(out=h_codes[a][:, cols].bitcast(E4M3), scales=h_scales[a][:, cols], in_=h[a, ch])
 
-        def quant_h_all(a):
-            nc.vector.quantize_mx(out=h_codes[a][:].bitcast(E4M3), scales=h_scales[a][:], in_=h0[:])
+        def quant_h_half(a, half):
+            cols = slice(half * 2 * CH, (half + 1) * 2 * CH)
+            nc.vector.quantize_mx(out=h_codes[a][:, cols].bitcast(E4M3), scales=h_scales[a][:, cols], in_=h_half[a, half][:])
 
         y_bank = {}
 
@@ -199,7 +203,7 @@ def tile_mix_bilin_fm_silu_kernel(tc, x, wx, c, wc, w_words, w_scales, b, out):
 
         def y_half(a, half, pair):
             if a == 0:
-                y_bank[half, pair] = bank(3 * half + pair)
+                y_bank[half, pair] = bank(CHUNKS * (pair // 2) + 2 * half + pair % 2)
             for n2 in range(2):
                 for c2 in range(2):
                     ch = 2 * half + c2
@@ -213,13 +217,9 @@ def tile_mix_bilin_fm_silu_kernel(tc, x, wx, c, wc, w_words, w_scales, b, out):
                         a == 1 and n2 == 1 and c2 == 1,
                     )
 
-        def y_full(a, nt):
-            if a == 0:
-                y_bank[nt] = bank(nt)
-            y_mm(y_bank[nt][:], a, nt, slice(0, T), a == 0, a == 1)
-
-        def finish_half(half, pair):
+        def finish_half(half, pair, singly=False):
             res = keep.tile([P, 2, 2 * CH], F32, name="res%d%d" % (half, pair))
+            tcols = slice(half * 2 * CH, (half + 1) * 2 * CH)
             for n2 in range(2):
                 nt = 2 * pair + n2
                 nc.scalar.activation(
@@ -228,88 +228,82 @@ def tile_mix_bilin_fm_silu_kernel(tc, x, wx, c, wc, w_words, w_scales, b, out):
                     func=mybir.ActivationFunctionType.Silu,
                     bias=bias[:, nt : nt + 1],
                 )
-            nc.sync.dma_start(
-                out=out[2 * pair * P : 2 * (pair + 1) * P, half * 2 * CH : (half + 1) * 2 * CH].rearrange("(n p) t -> p n t", p=P),
-                in_=res[:],
-            )
-
-        def finish_full(nt):
-            res = keep.tile([P, T], F32, name="res%d" % nt)
-            nc.scalar.activation(
-                out=res[:], in_=y_bank[nt][:], func=mybir.ActivationFunctionType.Silu, bias=bias[:, nt : nt + 1]
-            )
-            nc.sync.dma_start(out=out[nt * P : (nt + 1) * P, :], in_=res[:])
+                if singly:
+                    nc.sync.dma_start(out=out[nt * P : (nt + 1) * P, tcols], in_=res[:, n2, :])
+            if not singly:
+                nc.sync.dma_start(
+                    out=out[2 * pair * P : 2 * (pair + 1) * P, tcols].rearrange("(n p) t -> p n t", p=P),
+                    in_=res[:],
+                )
 
         def place_bias():
-            b_t = bank(4)
+            b_t = bank(7)
             nc.tensor.transpose(b_t[:, 0:P], b_rows[:], ident[:])
             nc.vector.tensor_copy(out=bias[:], in_=b_t[:, 0 : M // P])
 
         interleave("c0", 320)
         quant_in("c0")
         interleave("wc00", 320)
+        interleave("wc01", 256)
         quant_in("wc00")
         pc_pass(0, 0)
-        interleave("c1", 320)
-        quant_in("c1")
-        place_bias()
-        interleave("wc10", 320)
+        quant_in("wc01")
+        pc_pass(0, 1)
+        interleave("wc10", 512)
+        interleave("wc11", 128)
         quant_in("wc10")
+        quant_in("wc11")
+        interleave("c1", 256)
+        quant_in("c1")
         pc_pass(1, 0)
+        pc_pass(1, 1)
+        pc_copy(0, 0)
         interleave("x0", 512)
-        pc_copy(0)
         quant_in("x0")
-        interleave("wx00", 384)
+        pc_copy(1, 2)
+        interleave("wx00", 512)
+        interleave("wx01", 192)
+        place_bias()
         quant_in("wx00")
         for ch in range(CHUNKS):
             px_pass(0, 0, ch)
-        interleave("x1", 320)
+        quant_in("wx01")
+        for ch in range(CHUNKS):
+            px_pass(0, 1, ch)
+        interleave("x1", 256)
         quant_in("x1")
         interleave("wx10", 320)
         quant_in("wx10")
         for ch in range(CHUNKS):
             px_pass(1, 0, ch)
-        mult(0, 0)
-        interleave("wc01", 64)
-        mult(0, 1)
-        mult(0, 2)
-        mult(0, 3)
-        quant_in("wc01")
-        pc_pass(0, 1)
-        interleave("wx01", 192)
-        quant_h_all(0)
-        quant_in("wx01")
-        for ch in range(CHUNKS):
-            px_pass(0, 1, ch)
-        interleave("wc11", 320)
-        quant_in("wc11")
-        pc_pass(1, 1)
         interleave("wx11", 320)
-        pc_copy_half(1, 0)
-        pc_copy_half(1, 1)
+        mult(0, 0)
         quant_in("wx11")
         for ch in range(CHUNKS):
             px_pass(1, 1, ch)
-        y_half(0, 0, 0)
-        y_half(0, 0, 1)
-        y_half(0, 0, 2)
+        mult(0, 1)
+        quant_h(0, 0)
+        quant_h(0, 1)
         mult(1, 0)
         mult(1, 1)
         quant_h(1, 0)
         quant_h(1, 1)
+        for pair in range(4):
+            y_half(0, 0, pair)
+        for pair in range(4):
+            y_half(1, 0, pair)
+            finish_half(0, pair, singly=(pair == 0))
+        mult(0, 2)
+        mult(0, 3)
         mult(1, 2)
+        quant_h_half(0, 1)
         mult(1, 3)
         quant_h(1, 2)
         quant_h(1, 3)
-        for pair in range(3):
-            y_half(1, 0, pair)
-            finish_half(0, pair)
-        for pair in range(3):
-            y_half(0, 1, pair)
-        for pair in range(3):
+        y_half(0, 1, 0)
+        y_half(0, 1, 1)
+        for pair in range(4):
+            if pair >= 2:
+                y_half(0, 1, pair)
             y_half(1, 1, pair)
-            finish_half(1, pair)
-        for nt in range(6, 8):
-            y_full(0, nt)
-            y_full(1, nt)
-            finish_full(nt)
+            finish_half(1, pair, singly=(pair in (0, 3)))

@@ -63,8 +63,8 @@ def tile_mix_bilin_fm_silu_kernel(tc, x, wx, c, wc, w_words, w_scales, b, out):
         load("c1", c[rows_of(1), :])
         load("x0", x[rows_of(0), :])
         load_whole("wx0", wx[rows_of(0), :])
-        load("x1", x[rows_of(1), :])
         load("wx10", wx[rows_of(1), rows_of(0)])
+        load("x1", x[rows_of(1), :])
         load("wx11", wx[rows_of(1), rows_of(1)])
         w_sc = w_scales.bitcast(I32)
         for q in range(4):
@@ -99,6 +99,36 @@ def tile_mix_bilin_fm_silu_kernel(tc, x, wx, c, wc, w_words, w_scales, b, out):
                 nc.vector.tensor_copy(out=d[:, 0:mv], in_=s[:, 0:mv])
             if mv < P:
                 nc.scalar.copy(out=d[:, mv:P], in_=s[:, mv:P])
+
+        def share_copy(d, s, mv):
+            if mv > 0:
+                nc.vector.tensor_copy(out=d[:, 0:mv], in_=s[:, 0:mv])
+            if mv < d.shape[1]:
+                nc.scalar.copy(out=d[:, mv:], in_=s[:, mv:])
+
+        def interleave_x_half(half, mv):
+            g = keep.tile([P, 2 * CH * PACK], BF16, name="grouped_x1%d" % half, align_bytes=64)
+            grouped["x1", half] = g
+            s = raw["x1"][:, :, half * 2 * CH : (half + 1) * 2 * CH].rearrange("p i (m j) -> p m i j", j=PACK)
+            share_copy(g[:].rearrange("p (m j i) -> p m i j", j=PACK, i=PACK), s, mv)
+
+        def interleave_w_pair(name, u, mv):
+            g = keep.tile([P, 2 * P * PACK], BF16, name="grouped_%s%d" % (name, u), align_bytes=64)
+            grouped[name, u] = g
+            s = raw[name].rearrange("p i (m u e) -> p u m i e", u=2, e=2)[:, u]
+            share_copy(g[:].rearrange("p (e m i) -> p m i e", e=2, i=PACK), s, mv)
+
+        def quant_part(name, src, cols):
+            if name not in codes:
+                codes[name] = keep.tile([P, PASS], U32, name="codes_" + name, align_bytes=64)
+                scales[name] = keep.tile([P, PASS], U8, name="scales_" + name, align_bytes=64)
+            nc.vector.quantize_mx(out=codes[name][:, cols].bitcast(E4M3), scales=scales[name][:, cols], in_=src)
+
+        def quant_x_half(half):
+            quant_part("x1", grouped["x1", half][:], slice(half * 2 * CH, (half + 1) * 2 * CH))
+
+        def quant_w_tile(name, j):
+            quant_part(name, grouped[name, j // 2][:, (j % 2) * PASS : (j % 2 + 1) * PASS], slice(j * P, (j + 1) * P))
 
         def quantize(name, src, width, fmt):
             cd = keep.tile([P, width], U32, name="codes_" + name, align_bytes=64)
@@ -142,13 +172,13 @@ def tile_mix_bilin_fm_silu_kernel(tc, x, wx, c, wc, w_words, w_scales, b, out):
 
         px_bank = {}
 
-        def px_pass(g, a, ch):
+        def px_pass(g, a, ch, tiles=range(PACK)):
             wname = "wx%d%d" % (g, a)
             xname = "x%d" % g
             if g == 0:
                 px_bank[a, ch] = bank(CHUNKS * a + ch)
             tcols = slice(ch * CH, (ch + 1) * CH)
-            for j in range(PACK):
+            for j in tiles:
                 cols = slice(j * P, (j + 1) * P)
                 nc.tensor.matmul_mx(
                     out=px_bank[a, ch][:, j * CH : (j + 1) * CH],
@@ -204,8 +234,8 @@ def tile_mix_bilin_fm_silu_kernel(tc, x, wx, c, wc, w_words, w_scales, b, out):
         def y_half(a, half, pair):
             if a == 0:
                 y_bank[half, pair] = bank(CHUNKS * (pair // 2) + 2 * half + pair % 2)
-            for n2 in range(2):
-                for c2 in range(2):
+            for c2 in range(2):
+                for n2 in range(2):
                     ch = 2 * half + c2
                     col = (2 * n2 + c2) * CH
                     y_mm(
@@ -270,29 +300,37 @@ def tile_mix_bilin_fm_silu_kernel(tc, x, wx, c, wc, w_words, w_scales, b, out):
         quant_in("wx01")
         for ch in range(CHUNKS):
             px_pass(0, 1, ch)
-        interleave("x1", 256)
-        quant_in("x1")
         interleave("wx10", 320)
         quant_in("wx10")
+        interleave_x_half(0, 40)
+        interleave_x_half(1, 40)
+        quant_x_half(0)
+        quant_x_half(1)
         for ch in range(CHUNKS):
             px_pass(1, 0, ch)
-        interleave("wx11", 320)
         mult(0, 0)
-        quant_in("wx11")
-        for ch in range(CHUNKS):
-            px_pass(1, 1, ch)
+        interleave_w_pair("wx11", 0, 80)
+        interleave_w_pair("wx11", 1, 80)
+        for j in range(PACK):
+            quant_w_tile("wx11", j)
+        for half in range(2):
+            for j in range(PACK):
+                for ch in (2 * half, 2 * half + 1):
+                    px_pass(1, 1, ch, [j])
         mult(0, 1)
         quant_h(0, 0)
-        quant_h(0, 1)
         mult(1, 0)
+        quant_h(0, 1)
         mult(1, 1)
         quant_h(1, 0)
         quant_h(1, 1)
+        y_half(0, 0, 0)
+        y_half(0, 0, 1)
         for pair in range(4):
-            y_half(0, 0, pair)
-        for pair in range(4):
+            if pair >= 2:
+                y_half(0, 0, pair)
             y_half(1, 0, pair)
-            finish_half(0, pair, singly=(pair == 0))
+            finish_half(0, pair, singly=True)
         mult(0, 2)
         mult(0, 3)
         mult(1, 2)
@@ -306,4 +344,4 @@ def tile_mix_bilin_fm_silu_kernel(tc, x, wx, c, wc, w_words, w_scales, b, out):
             if pair >= 2:
                 y_half(0, 1, pair)
             y_half(1, 1, pair)
-            finish_half(1, pair, singly=(pair in (0, 3)))
+            finish_half(1, pair, singly=True)

@@ -59,8 +59,8 @@ def tile_mix_bilin_fm_silu_kernel(tc, x, wx, c, wc, w_words, w_scales, b, out):
 
         load("c0", c[rows_of(0), :])
         load_whole("wc0", wc[rows_of(0), :])
-        load_whole("wc1", wc[rows_of(1), :])
         load("c1", c[rows_of(1), :])
+        load_whole("wc1", wc[rows_of(1), :])
         load("x0", x[rows_of(0), :])
         load_whole("wx0", wx[rows_of(0), :])
         load("wx10", wx[rows_of(1), rows_of(0)])
@@ -106,10 +106,10 @@ def tile_mix_bilin_fm_silu_kernel(tc, x, wx, c, wc, w_words, w_scales, b, out):
             if mv < d.shape[1]:
                 nc.scalar.copy(out=d[:, mv:], in_=s[:, mv:])
 
-        def interleave_x_half(half, mv):
-            g = keep.tile([P, 2 * CH * PACK], BF16, name="grouped_x1%d" % half, align_bytes=64)
-            grouped["x1", half] = g
-            s = raw["x1"][:, :, half * 2 * CH : (half + 1) * 2 * CH].rearrange("p i (m j) -> p m i j", j=PACK)
+        def interleave_x_part(t0, t1, mv):
+            g = keep.tile([P, (t1 - t0) * PACK], BF16, name="grouped_x1%d" % t0, align_bytes=64)
+            grouped["x1", t0] = g
+            s = raw["x1"][:, :, t0:t1].rearrange("p i (m j) -> p m i j", j=PACK)
             share_copy(g[:].rearrange("p (m j i) -> p m i j", j=PACK, i=PACK), s, mv)
 
         def interleave_w_pair(name, u, mv):
@@ -124,8 +124,8 @@ def tile_mix_bilin_fm_silu_kernel(tc, x, wx, c, wc, w_words, w_scales, b, out):
                 scales[name] = keep.tile([P, PASS], U8, name="scales_" + name, align_bytes=64)
             nc.vector.quantize_mx(out=codes[name][:, cols].bitcast(E4M3), scales=scales[name][:, cols], in_=src)
 
-        def quant_x_half(half):
-            quant_part("x1", grouped["x1", half][:], slice(half * 2 * CH, (half + 1) * 2 * CH))
+        def quant_x_part(t0, t1):
+            quant_part("x1", grouped["x1", t0][:], slice(t0, t1))
 
         def quant_w_tile(name, j):
             quant_part(name, grouped[name, j // 2][:, (j % 2) * PASS : (j % 2 + 1) * PASS], slice(j * P, (j + 1) * P))
@@ -163,7 +163,7 @@ def tile_mix_bilin_fm_silu_kernel(tc, x, wx, c, wc, w_words, w_scales, b, out):
         def pc_copy(a, on_vector):
             whole = keep.tile([P, PACK, T], F32, name="pc%d" % a)
             for j in range(PACK):
-                if j < on_vector:
+                if j in on_vector:
                     nc.vector.tensor_copy(out=whole[:, j, :], in_=pc_bank[a, j][:])
                 else:
                     nc.scalar.copy(out=whole[:, j, :], in_=pc_bank[a, j][:])
@@ -204,9 +204,9 @@ def tile_mix_bilin_fm_silu_kernel(tc, x, wx, c, wc, w_words, w_scales, b, out):
                     h_half[a, ch // 2] = keep.tile([P, 2 * CH * PACK], BF16, name="h0%d" % (ch // 2), align_bytes=64)
                 h[a, ch] = h_half[a, ch // 2][:, (ch % 2) * CH * PACK : (ch % 2 + 1) * CH * PACK]
             nc.vector.tensor_tensor(
-                out=h[a, ch].rearrange("p (m i j) -> p m j i", i=PACK, j=PACK),
-                in0=px_bank[a, ch][:].rearrange("p (j m i) -> p m j i", j=PACK, i=PACK),
-                in1=pc[a, ch // 2][:, :, (ch % 2) * CH : (ch % 2 + 1) * CH].rearrange("p j (m i) -> p m j i", i=PACK),
+                out=h[a, ch].rearrange("p (m i j) -> p m j i", i=2, j=PACK),
+                in0=px_bank[a, ch][:].rearrange("p (j m i) -> p m j i", j=PACK, i=2),
+                in1=pc[a, ch // 2][:, :, (ch % 2) * CH : (ch % 2 + 1) * CH].rearrange("p j (m i) -> p m j i", i=2),
                 op=mybir.AluOpType.mult,
             )
 
@@ -279,38 +279,42 @@ def tile_mix_bilin_fm_silu_kernel(tc, x, wx, c, wc, w_words, w_scales, b, out):
         pc_pass(0, 0)
         quant_in("wc01")
         pc_pass(0, 1)
-        interleave("wc10", 512)
-        interleave("wc11", 128)
-        quant_in("wc10")
-        quant_in("wc11")
-        interleave("c1", 256)
+        interleave("c1", 320)
         quant_in("c1")
+        interleave("wc10", 320)
+        interleave("wc11", 256)
+        quant_in("wc10")
         pc_pass(1, 0)
+        quant_in("wc11")
         pc_pass(1, 1)
-        pc_copy(0, 0)
+        pc_copy(0, ())
         interleave("x0", 512)
         quant_in("x0")
-        pc_copy(1, 2)
+        pc_copy(1, (0, 2))
         interleave("wx00", 512)
-        interleave("wx01", 192)
+        interleave("wx01", 128)
         place_bias()
         quant_in("wx00")
         for ch in range(CHUNKS):
             px_pass(0, 0, ch)
         quant_in("wx01")
-        for ch in range(CHUNKS):
+        for ch in range(2):
             px_pass(0, 1, ch)
         interleave("wx10", 320)
         quant_in("wx10")
-        interleave_x_half(0, 40)
-        interleave_x_half(1, 40)
-        quant_x_half(0)
-        quant_x_half(1)
+        interleave_x_part(0, CH, CH // PACK)
+        interleave_x_part(CH, 2 * CH, CH // PACK)
+        interleave_x_part(2 * CH, T, 0)
+        quant_x_part(0, CH)
+        quant_x_part(CH, 2 * CH)
+        quant_x_part(2 * CH, T)
         for ch in range(CHUNKS):
             px_pass(1, 0, ch)
+        for ch in range(2, CHUNKS):
+            px_pass(0, 1, ch)
         mult(0, 0)
-        interleave_w_pair("wx11", 0, 80)
-        interleave_w_pair("wx11", 1, 80)
+        interleave_w_pair("wx11", 0, 84)
+        interleave_w_pair("wx11", 1, 84)
         for j in range(PACK):
             quant_w_tile("wx11", j)
         for half in range(2):

@@ -20,6 +20,8 @@ PACK = 4
 PASS = P * PACK
 CH = 128
 CHUNKS = T // CH
+TILES = M // P
+BANK = 512
 
 
 def tile_mix_bilin_fm_silu_kernel(tc, x, wx, c, wc, w_words, w_scales, b, out):
@@ -31,74 +33,62 @@ def tile_mix_bilin_fm_silu_kernel(tc, x, wx, c, wc, w_words, w_scales, b, out):
         ctx.enter_context(tc.manual_schedule())
 
         def bank(i):
-            return psum.tile([P, PASS], F32, name="bank%d" % i)
+            return psum.tile([P, BANK], F32, name="bank%d" % i)
 
         b_rows = keep.tile([P, P], F32, name="b_rows")
         ident = keep.tile([P, P], F32, name="ident")
         w_plane = keep.tile([P, 2, M], U8, name="w_plane", align_bytes=64)
+        bias = keep.tile([P, TILES], F32, name="bias")
         nc.gpsimd.memset(b_rows[:], 0.0)
         nc.gpsimd.memset(w_plane[:].rearrange("p a n -> p (a n)").bitcast(I32), 0)
         make_identity(nc, ident[:])
-        nc.scalar.dma_start(out=b_rows[0 : M // P, :], in_=b.rearrange("(i p) -> i p", p=P))
+        nc.scalar.dma_start(out=b_rows[0:TILES, :], in_=b.rearrange("(i p) -> i p", p=P))
 
         raw = {}
-
-        def load(name, rows):
-            t = keep.tile([P, PACK, PASS], F32, name="raw_" + name)
-            nc.sync.dma_start(out=t[:], in_=rows.rearrange("(p i) w -> p i w", i=PACK))
-            raw[name] = t[:]
-
-        def rows_of(g):
-            return slice(g * PASS, (g + 1) * PASS)
-
-        def load_whole(name, rows):
-            t = keep.tile([P, PACK, R], F32, name="raw_" + name)
-            nc.sync.dma_start(out=t[:], in_=rows.rearrange("(p i) w -> p i w", i=PACK))
-            for a in range(2):
-                raw[name + str(a)] = t[:, :, rows_of(a)]
-
-        load("c0", c[rows_of(0), :])
-        load_whole("wc0", wc[rows_of(0), :])
-        load("c1", c[rows_of(1), :])
-        load_whole("wc1", wc[rows_of(1), :])
-        load("x0", x[rows_of(0), :])
-        load_whole("wx0", wx[rows_of(0), :])
-        load("wx10", wx[rows_of(1), rows_of(0)])
-        load("x1", x[rows_of(1), :])
-        load("wx11", wx[rows_of(1), rows_of(1)])
-        w_sc = w_scales.bitcast(I32)
-        for q in range(4):
-            nc.sync.dma_start(
-                out=w_plane[32 * q : 32 * q + 4, :, :].bitcast(I32),
-                in_=w_sc[:, 4 * q : 4 * q + 4, :].rearrange("a q n -> q a n"),
-            )
-        w_codes = []
-        for a in range(2):
-            t = keep.tile([P, 2 * M], U8, name="w_codes%d" % a, align_bytes=64)
-            nc.sync.dma_start(out=t[:].bitcast(I32), in_=w_words[a].bitcast(I32))
-            w_codes.append(t)
-
-        bias = keep.tile([P, M // P], F32, name="bias")
-
         grouped = {}
         codes = {}
         scales = {}
+        w_codes = {}
+        w_half = {}
 
-        def interleave(name, cols_v):
-            src = raw[name]
-            g = stage.tile([P, PASS * PACK], BF16, name="grouped", align_bytes=64)
-            grouped[name] = g
-            if name[0] == "w":
-                s = src.rearrange("p i (m j) -> p m i j", j=PACK)
-                d = g[:].rearrange("p (j m i) -> p m i j", j=PACK, i=PACK)
-            else:
-                s = src.rearrange("p i (m j) -> p m i j", j=PACK)
-                d = g[:].rearrange("p (m j i) -> p m i j", j=PACK, i=PACK)
-            mv = cols_v // PACK
-            if mv > 0:
-                nc.vector.tensor_copy(out=d[:, 0:mv], in_=s[:, 0:mv])
-            if mv < P:
-                nc.scalar.copy(out=d[:, mv:P], in_=s[:, mv:P])
+        def span(g):
+            return slice(g * PASS, (g + 1) * PASS)
+
+        def load(name, rows):
+            t = keep.tile([P, PACK, rows.shape[1]], F32, name="raw_" + name)
+            nc.sync.dma_start(out=t[:], in_=rows.rearrange("(p i) w -> p i w", i=PACK))
+            raw[name] = t[:]
+
+        def load_whole(name, rows):
+            load(name, rows)
+            for a in range(2):
+                raw[name + str(a)] = raw[name][:, :, span(a)]
+
+        def load_w_scales():
+            w_sc = w_scales.bitcast(I32)
+            for r in range(4):
+                nc.sync.dma_start(
+                    out=w_plane[r:P:32, :, :].bitcast(I32),
+                    in_=w_sc[:, r:16:4, :].rearrange("a q n -> q a n"),
+                )
+
+        def load_w_codes(a):
+            w_codes[a] = keep.tile([P, 2 * M], U8, name="w_codes%d" % a, align_bytes=64)
+            nc.sync.dma_start(out=w_codes[a][:].bitcast(I32), in_=w_words[a].bitcast(I32))
+
+        def load_w_half(u):
+            t = keep.tile([P, 2, M], U8, name="w_half%d" % u, align_bytes=64)
+            nc.sync.dma_start(out=t[:].bitcast(I32), in_=w_words[:, :, u * M : (u + 1) * M].bitcast(I32).rearrange("a p n -> p a n"))
+            w_half[u] = t
+
+        def w_tile(a, nt):
+            if w_half:
+                return w_half[nt // 4][:, a, 2 * (nt % 4) * P : 2 * (nt % 4 + 1) * P]
+            return w_codes[a][:, 2 * nt * P : 2 * (nt + 1) * P]
+
+        def load_bias():
+            with nc.allow_non_contiguous_dma(reason="one bias value for each partition and output tile"):
+                nc.sync.dma_start(out=bias[:], in_=b.rearrange("(i p) -> p i", p=P))
 
         def share_copy(d, s, mv):
             if mv > 0:
@@ -106,10 +96,16 @@ def tile_mix_bilin_fm_silu_kernel(tc, x, wx, c, wc, w_words, w_scales, b, out):
             if mv < d.shape[1]:
                 nc.scalar.copy(out=d[:, mv:], in_=s[:, mv:])
 
-        def interleave_x_part(t0, t1, mv):
-            g = keep.tile([P, (t1 - t0) * PACK], BF16, name="grouped_x1%d" % t0, align_bytes=64)
-            grouped["x1", t0] = g
-            s = raw["x1"][:, :, t0:t1].rearrange("p i (m j) -> p m i j", j=PACK)
+        def interleave(name, mv):
+            g = stage.tile([P, PASS * PACK], BF16, name="grouped", align_bytes=64)
+            grouped[name] = g
+            order = "p (j m i) -> p m i j" if name[0] == "w" else "p (m j i) -> p m i j"
+            share_copy(g[:].rearrange(order, j=PACK, i=PACK), raw[name].rearrange("p i (m j) -> p m i j", j=PACK), mv)
+
+        def interleave_x(name, src, c0, c1, mv):
+            g = keep.tile([P, (c1 - c0) * PACK], BF16, name="grouped_" + name, align_bytes=64)
+            grouped[name] = g
+            s = raw[src][:, :, c0:c1].rearrange("p i (m j) -> p m i j", j=PACK)
             share_copy(g[:].rearrange("p (m j i) -> p m i j", j=PACK, i=PACK), s, mv)
 
         def interleave_w_pair(name, u, mv):
@@ -118,27 +114,31 @@ def tile_mix_bilin_fm_silu_kernel(tc, x, wx, c, wc, w_words, w_scales, b, out):
             s = raw[name].rearrange("p i (m u e) -> p u m i e", u=2, e=2)[:, u]
             share_copy(g[:].rearrange("p (e m i) -> p m i e", e=2, i=PACK), s, mv)
 
-        def quant_part(name, src, cols):
+        def interleave_w_half(name, mv):
+            g = keep.tile([P, PASS * PACK // 2], BF16, name="grouped_" + name, align_bytes=64)
+            grouped[name] = g
+            s = raw[name].rearrange("p i (m j) -> p m i j", j=PACK)
+            share_copy(g[:].rearrange("p (j m i) -> p m i j", j=PACK, i=PACK), s, mv)
+
+        def quant_w_half(dst, name, u, j):
+            half = P // 2
+            quant_into(dst, grouped[name][:, j * half * PACK : (j + 1) * half * PACK], slice(j * P + u * half, j * P + (u + 1) * half))
+
+        def quant_into(name, src, cols):
             if name not in codes:
                 codes[name] = keep.tile([P, PASS], U32, name="codes_" + name, align_bytes=64)
                 scales[name] = keep.tile([P, PASS], U8, name="scales_" + name, align_bytes=64)
-            nc.vector.quantize_mx(out=codes[name][:, cols].bitcast(E4M3), scales=scales[name][:, cols], in_=src)
-
-        def quant_x_part(t0, t1):
-            quant_part("x1", grouped["x1", t0][:], slice(t0, t1))
-
-        def quant_w_tile(name, j):
-            quant_part(name, grouped[name, j // 2][:, (j % 2) * PASS : (j % 2 + 1) * PASS], slice(j * P, (j + 1) * P))
-
-        def quantize(name, src, width, fmt):
-            cd = keep.tile([P, width], U32, name="codes_" + name, align_bytes=64)
-            sc = keep.tile([P, width], U8, name="scales_" + name, align_bytes=64)
-            nc.vector.quantize_mx(out=cd[:].bitcast(fmt), scales=sc[:], in_=src)
-            codes[name] = cd
-            scales[name] = sc
+            fmt = E5M2 if name[0] == "c" else E4M3
+            nc.vector.quantize_mx(out=codes[name][:, cols].bitcast(fmt), scales=scales[name][:, cols], in_=src)
 
         def quant_in(name):
-            quantize(name, grouped[name][:], PASS, E5M2 if name[0] == "c" else E4M3)
+            quant_into(name, grouped[name][:], slice(0, PASS))
+
+        def quant_x(dst, name, t0, t1):
+            quant_into(dst, grouped[name][:], slice(t0, t1))
+
+        def quant_w_tile(name, j):
+            quant_into(name, grouped[name, j // 2][:, (j % 2) * PASS : (j % 2 + 1) * PASS], slice(j * P, (j + 1) * P))
 
         pc_bank = {}
         pc = {}
@@ -161,22 +161,20 @@ def tile_mix_bilin_fm_silu_kernel(tc, x, wx, c, wc, w_words, w_scales, b, out):
                 )
 
         def pc_copy(a, on_vector):
-            whole = keep.tile([P, PACK, T], F32, name="pc%d" % a)
+            pc[a] = keep.tile([P, PACK, T], F32, name="pc%d" % a)
             for j in range(PACK):
                 if j in on_vector:
-                    nc.vector.tensor_copy(out=whole[:, j, :], in_=pc_bank[a, j][:])
+                    nc.vector.tensor_copy(out=pc[a][:, j, :], in_=pc_bank[a, j][:])
                 else:
-                    nc.scalar.copy(out=whole[:, j, :], in_=pc_bank[a, j][:])
-            for half in range(2):
-                pc[a, half] = whole[:, :, half * 2 * CH : (half + 1) * 2 * CH]
+                    nc.scalar.copy(out=pc[a][:, j, :], in_=pc_bank[a, j][:])
 
         px_bank = {}
 
-        def px_pass(g, a, ch, tiles=range(PACK)):
+        def px_pass(g, a, ch, tiles=range(PACK), at=None):
             wname = "wx%d%d" % (g, a)
             xname = "x%d" % g
             if g == 0:
-                px_bank[a, ch] = bank(CHUNKS * a + ch)
+                px_bank[a, ch] = bank(CHUNKS * a + ch if at is None else at)
             tcols = slice(ch * CH, (ch + 1) * CH)
             for j in tiles:
                 cols = slice(j * P, (j + 1) * P)
@@ -191,39 +189,32 @@ def tile_mix_bilin_fm_silu_kernel(tc, x, wx, c, wc, w_words, w_scales, b, out):
                 )
 
         h = {}
-        h_half = {}
         h_codes = [keep.tile([P, T], U32, name="h_codes%d" % a, align_bytes=64) for a in range(2)]
         h_scales = [keep.tile([P, T], U8, name="h_scales%d" % a, align_bytes=64) for a in range(2)]
 
         def mult(a, ch):
-            if a == 1 or ch < 2:
-                t = keep.tile([P, CH * PACK], BF16, name="hc%d%d" % (a, ch), align_bytes=64)
-                h[a, ch] = t[:]
-            else:
-                if ch % 2 == 0:
-                    h_half[a, ch // 2] = keep.tile([P, 2 * CH * PACK], BF16, name="h0%d" % (ch // 2), align_bytes=64)
-                h[a, ch] = h_half[a, ch // 2][:, (ch % 2) * CH * PACK : (ch % 2 + 1) * CH * PACK]
+            h[a, ch] = keep.tile([P, CH * PACK], BF16, name="h%d%d" % (a, ch), align_bytes=64)
             nc.vector.tensor_tensor(
-                out=h[a, ch].rearrange("p (m i j) -> p m j i", i=2, j=PACK),
+                out=h[a, ch][:].rearrange("p (m i j) -> p m j i", i=2, j=PACK),
                 in0=px_bank[a, ch][:].rearrange("p (j m i) -> p m j i", j=PACK, i=2),
-                in1=pc[a, ch // 2][:, :, (ch % 2) * CH : (ch % 2 + 1) * CH].rearrange("p j (m i) -> p m j i", i=2),
+                in1=pc[a][:, :, ch * CH : (ch + 1) * CH].rearrange("p j (m i) -> p m j i", i=2),
                 op=mybir.AluOpType.mult,
             )
 
         def quant_h(a, ch):
             cols = slice(ch * CH, (ch + 1) * CH)
-            nc.vector.quantize_mx(out=h_codes[a][:, cols].bitcast(E4M3), scales=h_scales[a][:, cols], in_=h[a, ch])
-
-        def quant_h_half(a, half):
-            cols = slice(half * 2 * CH, (half + 1) * 2 * CH)
-            nc.vector.quantize_mx(out=h_codes[a][:, cols].bitcast(E4M3), scales=h_scales[a][:, cols], in_=h_half[a, half][:])
+            nc.vector.quantize_mx(out=h_codes[a][:, cols].bitcast(E4M3), scales=h_scales[a][:, cols], in_=h[a, ch][:])
 
         y_bank = {}
 
-        def y_mm(dst, a, nt, cols, start, stop):
+        def y_open(key, at):
+            y_bank[key] = bank(at)
+
+        def y_mm(key, col, a, nt, t0, width, start=False, stop=False):
+            cols = slice(t0, t0 + width)
             nc.tensor.matmul_mx(
-                out=dst,
-                lhsT=w_codes[a][:, 2 * nt * P : 2 * (nt + 1) * P].bitcast(E2M1),
+                out=y_bank[key][:, col : col + width],
+                lhsT=w_tile(a, nt).bitcast(E2M1),
                 lhsT_scale=w_plane[:, a, nt * P : (nt + 1) * P],
                 rhs=h_codes[a][:, cols].bitcast(E4M3),
                 rhs_scale=h_scales[a][:, cols],
@@ -231,121 +222,158 @@ def tile_mix_bilin_fm_silu_kernel(tc, x, wx, c, wc, w_words, w_scales, b, out):
                 stop=stop,
             )
 
-        def y_half(a, half, pair):
+        def y_pass(a, t0, width, first, at=None):
+            count = BANK // width
             if a == 0:
-                y_bank[half, pair] = bank(CHUNKS * (pair // 2) + 2 * half + pair % 2)
-            for c2 in range(2):
-                for n2 in range(2):
-                    ch = 2 * half + c2
-                    col = (2 * n2 + c2) * CH
-                    y_mm(
-                        y_bank[half, pair][:, col : col + CH],
-                        a,
-                        2 * pair + n2,
-                        slice(ch * CH, (ch + 1) * CH),
-                        a == 0 and n2 == 0 and c2 == 0,
-                        a == 1 and n2 == 1 and c2 == 1,
-                    )
+                y_open((t0, first), at)
+            for i in range(count):
+                y_mm((t0, first), i * width, a, first + i, t0, width, a == 0 and i == 0, a == 1 and i == count - 1)
 
-        def finish_half(half, pair, singly=False):
-            res = keep.tile([P, 2, 2 * CH], F32, name="res%d%d" % (half, pair))
-            tcols = slice(half * 2 * CH, (half + 1) * 2 * CH)
-            for n2 in range(2):
-                nt = 2 * pair + n2
+        def finish(t0, width, first, group=1, count=None):
+            count = count or BANK // width
+            res = keep.tile([P, count, width], F32, name="res%d_%d" % (t0, first))
+            for i in range(count):
+                nt = first + i
                 nc.scalar.activation(
-                    out=res[:, n2, :],
-                    in_=y_bank[half, pair][:, n2 * 2 * CH : (n2 + 1) * 2 * CH],
+                    out=res[:, i, :],
+                    in_=y_bank[t0, first][:, i * width : (i + 1) * width],
                     func=mybir.ActivationFunctionType.Silu,
                     bias=bias[:, nt : nt + 1],
                 )
-                if singly:
-                    nc.sync.dma_start(out=out[nt * P : (nt + 1) * P, tcols], in_=res[:, n2, :])
-            if not singly:
-                nc.sync.dma_start(
-                    out=out[2 * pair * P : 2 * (pair + 1) * P, tcols].rearrange("(n p) t -> p n t", p=P),
-                    in_=res[:],
-                )
+                if (i + 1) % group == 0:
+                    n0 = nt + 1 - group
+                    nc.sync.dma_start(
+                        out=out[n0 * P : (nt + 1) * P, t0 : t0 + width].rearrange("(n p) t -> p n t", p=P),
+                        in_=res[:, i + 1 - group : i + 1, :],
+                    )
 
         def place_bias():
             b_t = bank(7)
             nc.tensor.transpose(b_t[:, 0:P], b_rows[:], ident[:])
-            nc.vector.tensor_copy(out=bias[:], in_=b_t[:, 0 : M // P])
+            nc.scalar.copy(out=bias[:], in_=b_t[:, 0:TILES])
 
-        interleave("c0", 320)
+        load("c0", c[span(0), :])
+        load_whole("wc0", wc[span(0), :])
+        load("c1", c[span(1), :])
+        load_whole("wc1", wc[span(1), :])
+        load_whole("wx0", wx[span(0), :])
+        load("x0", x[span(0), :])
+        load("wx10", wx[span(1), span(0)])
+        load("x1A", x[span(1), 0 : 2 * CH])
+        load("wx11a", wx[span(1), 512:768])
+        load("wx11b", wx[span(1), 768:1024])
+        load("x1C", x[span(1), 2 * CH : 3 * CH])
+        load("x1D", x[span(1), 3 * CH : T])
+        load_w_scales()
+        load_w_half(0)
+        load_w_half(1)
+        interleave("c0", 80)
         quant_in("c0")
-        interleave("wc00", 320)
-        interleave("wc01", 256)
+        interleave("wc00", 80)
+        interleave("wc01", 64)
         quant_in("wc00")
         pc_pass(0, 0)
         quant_in("wc01")
         pc_pass(0, 1)
-        interleave("c1", 320)
+        interleave("c1", 80)
         quant_in("c1")
-        interleave("wc10", 320)
-        interleave("wc11", 256)
+        interleave("wc10", 80)
+        interleave("wc11", 64)
         quant_in("wc10")
         pc_pass(1, 0)
         quant_in("wc11")
         pc_pass(1, 1)
-        pc_copy(0, ())
-        interleave("x0", 512)
-        quant_in("x0")
-        pc_copy(1, (0, 2))
-        interleave("wx00", 512)
-        interleave("wx01", 128)
-        place_bias()
+        pc_copy(0, (1, 3))
+        pc_copy(1, ())
+        interleave("wx00", 128)
         quant_in("wx00")
-        for ch in range(CHUNKS):
-            px_pass(0, 0, ch)
-        quant_in("wx01")
-        for ch in range(2):
-            px_pass(0, 1, ch)
-        interleave("wx10", 320)
-        quant_in("wx10")
-        interleave_x_part(0, CH, CH // PACK)
-        interleave_x_part(CH, 2 * CH, CH // PACK)
-        interleave_x_part(2 * CH, T, 0)
-        quant_x_part(0, CH)
-        quant_x_part(CH, 2 * CH)
-        quant_x_part(2 * CH, T)
-        for ch in range(CHUNKS):
-            px_pass(1, 0, ch)
-        for ch in range(2, CHUNKS):
-            px_pass(0, 1, ch)
-        mult(0, 0)
-        interleave_w_pair("wx11", 0, 84)
-        interleave_w_pair("wx11", 1, 84)
+        interleave_x("x0a", "x0", 0, 2 * CH, 64)
+        interleave_x("x0b", "x0", 2 * CH, T, 0)
+        place_bias()
+        quant_x("x0", "x0a", 0, 2 * CH)
+        px_pass(0, 0, 0)
+        px_pass(0, 0, 1)
+        interleave("wx01", 96)
+        quant_x("x0", "x0b", 2 * CH, T)
+        px_pass(0, 0, 2)
+        px_pass(0, 0, 3)
+        interleave_w_pair("wx10", 0, 84)
+        interleave_w_pair("wx10", 1, 84)
         for j in range(PACK):
-            quant_w_tile("wx11", j)
-        for half in range(2):
-            for j in range(PACK):
-                for ch in (2 * half, 2 * half + 1):
-                    px_pass(1, 1, ch, [j])
+            quant_w_tile("wx10", j)
+        interleave_x("x1a", "x1A", 0, CH, 32)
+        interleave_x("x1b", "x1A", CH, 2 * CH, 0)
+        quant_x("x1", "x1a", 0, CH)
+        quant_x("x1", "x1b", CH, 2 * CH)
+        quant_in("wx01")
+        px_pass(1, 0, 0)
+        px_pass(1, 0, 1)
+        px_pass(0, 1, 0)
+        px_pass(0, 1, 1)
+        px_pass(0, 1, 2)
+        interleave_w_half("wx11a", 0)
+        mult(0, 0)
         mult(0, 1)
+        interleave_w_half("wx11b", 42)
+        for j in range(PACK):
+            quant_w_half("wx11", "wx11a", 0, j)
+        for j in range(PACK):
+            quant_w_half("wx11", "wx11b", 1, j)
+            px_pass(1, 1, 0, [j])
+        px_pass(1, 1, 1)
+        interleave_x("x1c", "x1C", 0, CH, 32)
+        interleave_x("x1d", "x1D", 0, CH, 0)
         quant_h(0, 0)
+        quant_x("x1", "x1c", 2 * CH, 3 * CH)
         mult(1, 0)
         quant_h(0, 1)
         mult(1, 1)
         quant_h(1, 0)
+        quant_x("x1", "x1d", 3 * CH, T)
         quant_h(1, 1)
-        y_half(0, 0, 0)
-        y_half(0, 0, 1)
-        for pair in range(4):
-            if pair >= 2:
-                y_half(0, 0, pair)
-            y_half(1, 0, pair)
-            finish_half(0, pair, singly=True)
+        px_pass(1, 0, 2)
+        px_pass(1, 1, 2)
+        px_pass(0, 1, 3)
+        y_open((0, 0), 0)
+        y_mm((0, 0), 0, 0, 0, 0, 256, start=True)
+        y_pass(0, 0, 256, 1, 1)
+        y_mm((0, 0), 0, 1, 0, 0, 128)
+        px_pass(1, 0, 3)
+        y_mm((0, 0), 128, 1, 0, 128, 128, stop=True)
+        finish(0, 256, 0, 1, 1)
+        y_pass(1, 0, 256, 1)
+        finish(0, 256, 1)
+        y_pass(0, 0, 256, 3, 4)
+        y_pass(1, 0, 256, 3)
+        finish(0, 256, 3)
+        px_pass(1, 1, 3)
         mult(0, 2)
-        mult(0, 3)
         mult(1, 2)
-        quant_h_half(0, 1)
-        mult(1, 3)
+        quant_h(0, 2)
         quant_h(1, 2)
+        mult(0, 3)
+        mult(1, 3)
+        quant_h(0, 3)
         quant_h(1, 3)
-        y_half(0, 1, 0)
-        y_half(0, 1, 1)
-        for pair in range(4):
-            if pair >= 2:
-                y_half(0, 1, pair)
-            y_half(1, 1, pair)
-            finish_half(1, pair, singly=True)
+        for nt in range(5, 8):
+            y_open((0, nt), [5, 0, 2][nt - 5])
+            for a in range(2):
+                y_mm((0, nt), 0, a, nt, 0, 256, start=(a == 0))
+            for a in range(2):
+                y_mm((0, nt), 256, a, nt, 256, 128, stop=(a == 1))
+            finish(0, 384, nt)
+        y_pass(0, 256, 256, 0, 1)
+        y_pass(1, 256, 256, 0)
+        finish(256, 256, 0)
+        y_pass(0, 256, 256, 2, 6)
+        y_pass(1, 256, 256, 2)
+        finish(256, 256, 2)
+        y_open((256, 4), 4)
+        y_mm((256, 4), 0, 0, 4, 256, 256, start=True)
+        y_mm((256, 4), 0, 1, 4, 256, 256, stop=True)
+        finish(256, 256, 4, 1, 1)
+        y_open((384, 5), 3)
+        for a in range(2):
+            for i in range(3):
+                y_mm((384, 5), 128 * i, a, 5 + i, 384, 128, start=(a == 0 and i == 0), stop=(a == 1 and i == 2))
+        finish(384, 128, 5, 1, 3)

@@ -39,8 +39,14 @@ def tile_mix_bilin_fm_silu_kernel(tc, x, wx, c, wc, w_words, w_scales, b, out):
         ident = keep.tile([P, P], F32, name="ident")
         w_plane = keep.tile([P, 2, M], U8, name="w_plane", align_bytes=64)
         bias = keep.tile([P, TILES], F32, name="bias")
-        nc.gpsimd.memset(b_rows[:], 0.0)
+        nc.vector.memset(b_rows[:], 0.0)
         nc.gpsimd.memset(w_plane[:].rearrange("p a n -> p (a n)").bitcast(I32), 0)
+        w_sc = w_scales.bitcast(I32)
+        for r in range(4):
+            nc.gpsimd.dma_start(
+                out=w_plane[r:P:32, :, :].bitcast(I32),
+                in_=w_sc[:, r:16:4, :].rearrange("a q n -> q a n"),
+            )
         make_identity(nc, ident[:])
         nc.scalar.dma_start(out=b_rows[0:TILES, :], in_=b.rearrange("(i p) -> i p", p=P))
 
@@ -63,14 +69,6 @@ def tile_mix_bilin_fm_silu_kernel(tc, x, wx, c, wc, w_words, w_scales, b, out):
             load(name, rows)
             for a in range(2):
                 raw[name + str(a)] = raw[name][:, :, span(a)]
-
-        def load_w_scales():
-            w_sc = w_scales.bitcast(I32)
-            for r in range(4):
-                nc.sync.dma_start(
-                    out=w_plane[r:P:32, :, :].bitcast(I32),
-                    in_=w_sc[:, r:16:4, :].rearrange("a q n -> q a n"),
-                )
 
         def load_w_codes(a):
             w_codes[a] = keep.tile([P, 2 * M], U8, name="w_codes%d" % a, align_bytes=64)
@@ -264,9 +262,8 @@ def tile_mix_bilin_fm_silu_kernel(tc, x, wx, c, wc, w_words, w_scales, b, out):
         load("wx11b", wx[span(1), 768:1024])
         load("x1C", x[span(1), 2 * CH : 3 * CH])
         load("x1D", x[span(1), 3 * CH : T])
-        load_w_scales()
-        load_w_half(0)
-        load_w_half(1)
+        load_w_codes(0)
+        load_w_codes(1)
         interleave("c0", 80)
         quant_in("c0")
         interleave("wc00", 80)
@@ -277,10 +274,10 @@ def tile_mix_bilin_fm_silu_kernel(tc, x, wx, c, wc, w_words, w_scales, b, out):
         pc_pass(0, 1)
         interleave("c1", 80)
         quant_in("c1")
-        interleave("wc10", 80)
-        interleave("wc11", 64)
+        interleave("wc10", 84)
         quant_in("wc10")
         pc_pass(1, 0)
+        interleave("wc11", 64)
         quant_in("wc11")
         pc_pass(1, 1)
         pc_copy(0, (1, 3))
@@ -293,7 +290,7 @@ def tile_mix_bilin_fm_silu_kernel(tc, x, wx, c, wc, w_words, w_scales, b, out):
         quant_x("x0", "x0a", 0, 2 * CH)
         px_pass(0, 0, 0)
         px_pass(0, 0, 1)
-        interleave("wx01", 96)
+        interleave("wx01", 68)
         quant_x("x0", "x0b", 2 * CH, T)
         px_pass(0, 0, 2)
         px_pass(0, 0, 3)
@@ -321,12 +318,12 @@ def tile_mix_bilin_fm_silu_kernel(tc, x, wx, c, wc, w_words, w_scales, b, out):
             quant_w_half("wx11", "wx11b", 1, j)
             px_pass(1, 1, 0, [j])
         px_pass(1, 1, 1)
-        interleave_x("x1c", "x1C", 0, CH, 32)
+        interleave_x("x1c", "x1C", 0, CH, 0)
         interleave_x("x1d", "x1D", 0, CH, 0)
         quant_h(0, 0)
+        quant_h(0, 1)
         quant_x("x1", "x1c", 2 * CH, 3 * CH)
         mult(1, 0)
-        quant_h(0, 1)
         mult(1, 1)
         quant_h(1, 0)
         quant_x("x1", "x1d", 3 * CH, T)

@@ -41,14 +41,11 @@ def tile_mix_bilin_fm_silu_kernel(tc, x, wx, c, wc, w_words, w_scales, b, out):
         bias = keep.tile([P, TILES], F32, name="bias")
         nc.vector.memset(b_rows[:], 0.0)
         nc.gpsimd.memset(w_plane[:].rearrange("p a n -> p (a n)").bitcast(I32), 0)
-        w_sc = w_scales.bitcast(I32)
-        for r in range(4):
-            nc.gpsimd.dma_start(
-                out=w_plane[r:P:32, :, :].bitcast(I32),
-                in_=w_sc[:, r:16:4, :].rearrange("a q n -> q a n"),
-            )
         make_identity(nc, ident[:])
         nc.scalar.dma_start(out=b_rows[0:TILES, :], in_=b.rearrange("(i p) -> i p", p=P))
+
+        warm = keep.tile([P, 1], F32, name="warm")
+        nc.scalar.activation(out=warm[:], in_=ident[:, 0:1], func=mybir.ActivationFunctionType.Silu)
 
         raw = {}
         grouped = {}
@@ -69,6 +66,14 @@ def tile_mix_bilin_fm_silu_kernel(tc, x, wx, c, wc, w_words, w_scales, b, out):
             load(name, rows)
             for a in range(2):
                 raw[name + str(a)] = raw[name][:, :, span(a)]
+
+        def load_w_scales():
+            w_sc = w_scales.bitcast(I32)
+            for r in range(4):
+                nc.sync.dma_start(
+                    out=w_plane[r:P:32, :, :].bitcast(I32),
+                    in_=w_sc[:, r:16:4, :].rearrange("a q n -> q a n"),
+                )
 
         def load_w_codes(a):
             w_codes[a] = keep.tile([P, 2 * M], U8, name="w_codes%d" % a, align_bytes=64)
@@ -262,6 +267,7 @@ def tile_mix_bilin_fm_silu_kernel(tc, x, wx, c, wc, w_words, w_scales, b, out):
         load("wx11b", wx[span(1), 768:1024])
         load("x1C", x[span(1), 2 * CH : 3 * CH])
         load("x1D", x[span(1), 3 * CH : T])
+        load_w_scales()
         load_w_codes(0)
         load_w_codes(1)
         interleave("c0", 80)

@@ -39,13 +39,10 @@ def tile_mix_bilin_fm_silu_kernel(tc, x, wx, c, wc, w_words, w_scales, b, out):
         ident = keep.tile([P, P], F32, name="ident")
         w_plane = keep.tile([P, 2, M], U8, name="w_plane", align_bytes=64)
         bias = keep.tile([P, TILES], F32, name="bias")
-        nc.vector.memset(b_rows[:], 0.0)
+        nc.gpsimd.memset(b_rows[:], 0.0)
         nc.gpsimd.memset(w_plane[:].rearrange("p a n -> p (a n)").bitcast(I32), 0)
         make_identity(nc, ident[:])
         nc.scalar.dma_start(out=b_rows[0:TILES, :], in_=b.rearrange("(i p) -> i p", p=P))
-
-        warm = keep.tile([P, 1], F32, name="warm")
-        nc.scalar.activation(out=warm[:], in_=ident[:, 0:1], func=mybir.ActivationFunctionType.Silu)
 
         raw = {}
         grouped = {}
@@ -78,6 +75,12 @@ def tile_mix_bilin_fm_silu_kernel(tc, x, wx, c, wc, w_words, w_scales, b, out):
         def load_w_codes(a):
             w_codes[a] = keep.tile([P, 2 * M], U8, name="w_codes%d" % a, align_bytes=64)
             nc.sync.dma_start(out=w_codes[a][:].bitcast(I32), in_=w_words[a].bitcast(I32))
+
+        def load_w_all():
+            t = keep.tile([P, 2, 2 * M], U8, name="w_codes", align_bytes=64)
+            nc.sync.dma_start(out=t[:].bitcast(I32), in_=w_words.bitcast(I32).rearrange("a p n -> p a n"))
+            for a in range(2):
+                w_codes[a] = t[:, a, :]
 
         def load_w_half(u):
             t = keep.tile([P, 2, M], U8, name="w_half%d" % u, align_bytes=64)
@@ -163,9 +166,10 @@ def tile_mix_bilin_fm_silu_kernel(tc, x, wx, c, wc, w_words, w_scales, b, out):
                     stop=(g == 1),
                 )
 
-        def pc_copy(a, on_vector):
-            pc[a] = keep.tile([P, PACK, T], F32, name="pc%d" % a)
-            for j in range(PACK):
+        def pc_copy(a, on_vector, tiles=range(PACK)):
+            if a not in pc:
+                pc[a] = keep.tile([P, PACK, T], F32, name="pc%d" % a)
+            for j in tiles:
                 if j in on_vector:
                     nc.vector.tensor_copy(out=pc[a][:, j, :], in_=pc_bank[a, j][:])
                 else:
@@ -251,7 +255,7 @@ def tile_mix_bilin_fm_silu_kernel(tc, x, wx, c, wc, w_words, w_scales, b, out):
                     )
 
         def place_bias():
-            b_t = bank(7)
+            b_t = bank(5)
             nc.tensor.transpose(b_t[:, 0:P], b_rows[:], ident[:])
             nc.scalar.copy(out=bias[:], in_=b_t[:, 0:TILES])
 
@@ -263,13 +267,10 @@ def tile_mix_bilin_fm_silu_kernel(tc, x, wx, c, wc, w_words, w_scales, b, out):
         load("x0", x[span(0), :])
         load("wx10", wx[span(1), span(0)])
         load("x1A", x[span(1), 0 : 2 * CH])
-        load("wx11a", wx[span(1), 512:768])
-        load("wx11b", wx[span(1), 768:1024])
-        load("x1C", x[span(1), 2 * CH : 3 * CH])
-        load("x1D", x[span(1), 3 * CH : T])
+        load("wx11", wx[span(1), span(1)])
+        load("x1B", x[span(1), 2 * CH : T])
+        load_w_all()
         load_w_scales()
-        load_w_codes(0)
-        load_w_codes(1)
         interleave("c0", 80)
         quant_in("c0")
         interleave("wc00", 80)
@@ -286,8 +287,8 @@ def tile_mix_bilin_fm_silu_kernel(tc, x, wx, c, wc, w_words, w_scales, b, out):
         interleave("wc11", 64)
         quant_in("wc11")
         pc_pass(1, 1)
-        pc_copy(0, (1, 3))
-        pc_copy(1, ())
+        pc_copy(0, (1,))
+        pc_copy(1, (), [0, 1])
         interleave("wx00", 128)
         quant_in("wx00")
         interleave_x("x0a", "x0", 0, 2 * CH, 64)
@@ -304,39 +305,39 @@ def tile_mix_bilin_fm_silu_kernel(tc, x, wx, c, wc, w_words, w_scales, b, out):
         interleave_w_pair("wx10", 1, 84)
         for j in range(PACK):
             quant_w_tile("wx10", j)
+        pc_copy(1, (), [2])
         interleave_x("x1a", "x1A", 0, CH, 32)
         interleave_x("x1b", "x1A", CH, 2 * CH, 0)
+        pc_copy(1, (), [3])
         quant_x("x1", "x1a", 0, CH)
         quant_x("x1", "x1b", CH, 2 * CH)
-        quant_in("wx01")
         px_pass(1, 0, 0)
         px_pass(1, 0, 1)
+        quant_in("wx01")
         px_pass(0, 1, 0)
         px_pass(0, 1, 1)
-        px_pass(0, 1, 2)
-        interleave_w_half("wx11a", 0)
         mult(0, 0)
-        mult(0, 1)
-        interleave_w_half("wx11b", 42)
+        px_pass(0, 1, 2)
+        interleave_w_pair("wx11", 0, 84)
+        interleave_w_pair("wx11", 1, 84)
         for j in range(PACK):
-            quant_w_half("wx11", "wx11a", 0, j)
-        for j in range(PACK):
-            quant_w_half("wx11", "wx11b", 1, j)
+            quant_w_tile("wx11", j)
             px_pass(1, 1, 0, [j])
         px_pass(1, 1, 1)
-        interleave_x("x1c", "x1C", 0, CH, 0)
-        interleave_x("x1d", "x1D", 0, CH, 0)
-        quant_h(0, 0)
-        quant_h(0, 1)
-        quant_x("x1", "x1c", 2 * CH, 3 * CH)
+        px_pass(0, 1, 3)
+        interleave_x("x1c", "x1B", 0, CH, 0)
+        interleave_x("x1d", "x1B", CH, 2 * CH, 0)
+        mult(0, 1)
         mult(1, 0)
+        quant_h(0, 0)
+        quant_x("x1", "x1c", 2 * CH, 3 * CH)
+        quant_h(0, 1)
         mult(1, 1)
         quant_h(1, 0)
         quant_x("x1", "x1d", 3 * CH, T)
         quant_h(1, 1)
         px_pass(1, 0, 2)
         px_pass(1, 1, 2)
-        px_pass(0, 1, 3)
         y_open((0, 0), 0)
         y_mm((0, 0), 0, 0, 0, 0, 256, start=True)
         y_pass(0, 0, 256, 1, 1)

@@ -64,11 +64,11 @@ def tile_mix_bilin_fm_silu_kernel(tc, x, wx, c, wc, w_words, w_scales, b, out):
             for a in range(2):
                 raw[name + str(a)] = raw[name][:, :, span(a)]
 
-        def load_w_scales():
-            w_sc = w_scales.bitcast(I32)
+        def load_w_scales(n0, n1):
+            w_sc = w_scales[:, :, n0:n1].bitcast(I32)
             for r in range(4):
                 nc.sync.dma_start(
-                    out=w_plane[r:P:32, :, :].bitcast(I32),
+                    out=w_plane[r:P:32, :, n0:n1].bitcast(I32),
                     in_=w_sc[:, r:16:4, :].rearrange("a q n -> q a n"),
                 )
 
@@ -82,15 +82,16 @@ def tile_mix_bilin_fm_silu_kernel(tc, x, wx, c, wc, w_words, w_scales, b, out):
             for a in range(2):
                 w_codes[a] = t[:, a, :]
 
-        def load_w_half(u):
-            t = keep.tile([P, 2, M], U8, name="w_half%d" % u, align_bytes=64)
-            nc.sync.dma_start(out=t[:].bitcast(I32), in_=w_words[:, :, u * M : (u + 1) * M].bitcast(I32).rearrange("a p n -> p a n"))
-            w_half[u] = t
+        def load_w_part(n0, n1):
+            for a in range(2):
+                t = keep.tile([P, 2 * (n1 - n0) * P], U8, name="w_part%d%d" % (a, n0), align_bytes=64)
+                nc.sync.dma_start(out=t[:].bitcast(I32), in_=w_words[a, :, 2 * n0 * P : 2 * n1 * P].bitcast(I32))
+                for nt in range(n0, n1):
+                    w_codes[a, nt] = t[:, 2 * (nt - n0) * P : 2 * (nt - n0 + 1) * P]
+            load_w_scales(n0 * P, n1 * P)
 
         def w_tile(a, nt):
-            if w_half:
-                return w_half[nt // 4][:, a, 2 * (nt % 4) * P : 2 * (nt % 4 + 1) * P]
-            return w_codes[a][:, 2 * nt * P : 2 * (nt + 1) * P]
+            return w_codes[a, nt]
 
         def load_bias():
             with nc.allow_non_contiguous_dma(reason="one bias value for each partition and output tile"):
@@ -269,8 +270,8 @@ def tile_mix_bilin_fm_silu_kernel(tc, x, wx, c, wc, w_words, w_scales, b, out):
         load("x1A", x[span(1), 0 : 2 * CH])
         load("wx11", wx[span(1), span(1)])
         load("x1B", x[span(1), 2 * CH : T])
-        load_w_all()
-        load_w_scales()
+        load_w_part(0, 3)
+        load_w_part(3, TILES)
         interleave("c0", 80)
         quant_in("c0")
         interleave("wc00", 80)
@@ -328,8 +329,8 @@ def tile_mix_bilin_fm_silu_kernel(tc, x, wx, c, wc, w_words, w_scales, b, out):
         interleave_x("x1c", "x1B", 0, CH, 0)
         interleave_x("x1d", "x1B", CH, 2 * CH, 0)
         mult(0, 1)
-        mult(1, 0)
         quant_h(0, 0)
+        mult(1, 0)
         quant_x("x1", "x1c", 2 * CH, 3 * CH)
         quant_h(0, 1)
         mult(1, 1)

@@ -37,7 +37,7 @@ def tile_mix_bilin_fm_silu_kernel(tc, x, wx, c, wc, w_words, w_scales, b, out):
 
         b_rows = keep.tile([P, P], F32, name="b_rows")
         ident = keep.tile([P, P], F32, name="ident")
-        w_plane = keep.tile([P, 2, M], U8, name="w_plane", align_bytes=64)
+        w_plane = keep.tile([P, 2, M], U8, name="w_plane", align_bytes=256)
         bias = keep.tile([P, TILES], F32, name="bias")
         nc.gpsimd.memset(b_rows[:], 0.0)
         nc.gpsimd.memset(w_plane[:].rearrange("p a n -> p (a n)").bitcast(I32), 0)
@@ -55,7 +55,7 @@ def tile_mix_bilin_fm_silu_kernel(tc, x, wx, c, wc, w_words, w_scales, b, out):
             return slice(g * PASS, (g + 1) * PASS)
 
         def load(name, rows):
-            t = keep.tile([P, PACK, rows.shape[1]], F32, name="raw_" + name)
+            t = keep.tile([P, PACK, rows.shape[1]], F32, name="raw_" + name, align_bytes=256)
             nc.sync.dma_start(out=t[:], in_=rows.rearrange("(p i) w -> p i w", i=PACK))
             raw[name] = t[:]
 
@@ -73,18 +73,18 @@ def tile_mix_bilin_fm_silu_kernel(tc, x, wx, c, wc, w_words, w_scales, b, out):
                 )
 
         def load_w_codes(a):
-            w_codes[a] = keep.tile([P, 2 * M], U8, name="w_codes%d" % a, align_bytes=64)
+            w_codes[a] = keep.tile([P, 2 * M], U8, name="w_codes%d" % a, align_bytes=256)
             nc.sync.dma_start(out=w_codes[a][:].bitcast(I32), in_=w_words[a].bitcast(I32))
 
         def load_w_all():
-            t = keep.tile([P, 2, 2 * M], U8, name="w_codes", align_bytes=64)
+            t = keep.tile([P, 2, 2 * M], U8, name="w_codes", align_bytes=256)
             nc.sync.dma_start(out=t[:].bitcast(I32), in_=w_words.bitcast(I32).rearrange("a p n -> p a n"))
             for a in range(2):
                 w_codes[a] = t[:, a, :]
 
         def load_w_part(n0, n1):
             for a in range(2):
-                t = keep.tile([P, 2 * (n1 - n0) * P], U8, name="w_part%d%d" % (a, n0), align_bytes=64)
+                t = keep.tile([P, 2 * (n1 - n0) * P], U8, name="w_part%d%d" % (a, n0), align_bytes=256)
                 nc.sync.dma_start(out=t[:].bitcast(I32), in_=w_words[a, :, 2 * n0 * P : 2 * n1 * P].bitcast(I32))
                 for nt in range(n0, n1):
                     w_codes[a, nt] = t[:, 2 * (nt - n0) * P : 2 * (nt - n0 + 1) * P]
@@ -104,25 +104,25 @@ def tile_mix_bilin_fm_silu_kernel(tc, x, wx, c, wc, w_words, w_scales, b, out):
                 nc.scalar.copy(out=d[:, mv:], in_=s[:, mv:])
 
         def interleave(name, mv):
-            g = stage.tile([P, PASS * PACK], BF16, name="grouped", align_bytes=64)
+            g = stage.tile([P, PASS * PACK], BF16, name="grouped", align_bytes=256)
             grouped[name] = g
             order = "p (j m i) -> p m i j" if name[0] == "w" else "p (m j i) -> p m i j"
             share_copy(g[:].rearrange(order, j=PACK, i=PACK), raw[name].rearrange("p i (m j) -> p m i j", j=PACK), mv)
 
         def interleave_x(name, src, c0, c1, mv):
-            g = keep.tile([P, (c1 - c0) * PACK], BF16, name="grouped_" + name, align_bytes=64)
+            g = keep.tile([P, (c1 - c0) * PACK], BF16, name="grouped_" + name, align_bytes=256)
             grouped[name] = g
             s = raw[src][:, :, c0:c1].rearrange("p i (m j) -> p m i j", j=PACK)
             share_copy(g[:].rearrange("p (m j i) -> p m i j", j=PACK, i=PACK), s, mv)
 
         def interleave_w_pair(name, u, mv):
-            g = keep.tile([P, 2 * P * PACK], BF16, name="grouped_%s%d" % (name, u), align_bytes=64)
+            g = keep.tile([P, 2 * P * PACK], BF16, name="grouped_%s%d" % (name, u), align_bytes=256)
             grouped[name, u] = g
             s = raw[name].rearrange("p i (m u e) -> p u m i e", u=2, e=2)[:, u]
             share_copy(g[:].rearrange("p (e m i) -> p m i e", e=2, i=PACK), s, mv)
 
         def interleave_w_half(name, mv):
-            g = keep.tile([P, PASS * PACK // 2], BF16, name="grouped_" + name, align_bytes=64)
+            g = keep.tile([P, PASS * PACK // 2], BF16, name="grouped_" + name, align_bytes=256)
             grouped[name] = g
             s = raw[name].rearrange("p i (m j) -> p m i j", j=PACK)
             share_copy(g[:].rearrange("p (j m i) -> p m i j", j=PACK, i=PACK), s, mv)
@@ -133,8 +133,8 @@ def tile_mix_bilin_fm_silu_kernel(tc, x, wx, c, wc, w_words, w_scales, b, out):
 
         def quant_into(name, src, cols):
             if name not in codes:
-                codes[name] = keep.tile([P, PASS], U32, name="codes_" + name, align_bytes=64)
-                scales[name] = keep.tile([P, PASS], U8, name="scales_" + name, align_bytes=64)
+                codes[name] = keep.tile([P, PASS], U32, name="codes_" + name, align_bytes=256)
+                scales[name] = keep.tile([P, PASS], U8, name="scales_" + name, align_bytes=256)
             fmt = E5M2 if name[0] == "c" else E4M3
             nc.vector.quantize_mx(out=codes[name][:, cols].bitcast(fmt), scales=scales[name][:, cols], in_=src)
 
@@ -197,11 +197,11 @@ def tile_mix_bilin_fm_silu_kernel(tc, x, wx, c, wc, w_words, w_scales, b, out):
                 )
 
         h = {}
-        h_codes = [keep.tile([P, T], U32, name="h_codes%d" % a, align_bytes=64) for a in range(2)]
-        h_scales = [keep.tile([P, T], U8, name="h_scales%d" % a, align_bytes=64) for a in range(2)]
+        h_codes = [keep.tile([P, T], U32, name="h_codes%d" % a, align_bytes=256) for a in range(2)]
+        h_scales = [keep.tile([P, T], U8, name="h_scales%d" % a, align_bytes=256) for a in range(2)]
 
         def mult(a, ch):
-            h[a, ch] = keep.tile([P, CH * PACK], BF16, name="h%d%d" % (a, ch), align_bytes=64)
+            h[a, ch] = keep.tile([P, CH * PACK], BF16, name="h%d%d" % (a, ch), align_bytes=256)
             nc.vector.tensor_tensor(
                 out=h[a, ch][:].rearrange("p (m i j) -> p m j i", i=2, j=PACK),
                 in0=px_bank[a, ch][:].rearrange("p (j m i) -> p m j i", j=PACK, i=2),
@@ -239,7 +239,7 @@ def tile_mix_bilin_fm_silu_kernel(tc, x, wx, c, wc, w_words, w_scales, b, out):
 
         def finish(t0, width, first, group=1, count=None):
             count = count or BANK // width
-            res = keep.tile([P, count, width], F32, name="res%d_%d" % (t0, first))
+            res = keep.tile([P, count, width], F32, name="res%d_%d" % (t0, first), align_bytes=256)
             for i in range(count):
                 nt = first + i
                 nc.scalar.activation(

@@ -37,13 +37,16 @@ def tile_mix_bilin_fm_silu_kernel(tc, x, wx, c, wc, w_words, w_scales, b, out):
 
         b_rows = keep.tile([P, P], F32, name="b_rows")
         ident = keep.tile([P, P], F32, name="ident")
-        w_plane = keep.tile([P, 2, M], U8, name="w_plane", align_bytes=256)
+        w_plane = keep.tile([P, 2, M], U8, name="w_plane", align_bytes=1024)
         bias = keep.tile([P, TILES], F32, name="bias")
         nc.gpsimd.memset(b_rows[:], 0.0)
         nc.gpsimd.memset(w_plane[:].rearrange("p a n -> p (a n)").bitcast(I32), 0)
         make_identity(nc, ident[:])
         nc.scalar.dma_start(out=b_rows[0:TILES, :], in_=b.rearrange("(i p) -> i p", p=P))
 
+        raw_all = keep.tile([P, 2 * (R + T) * K // P], F32, name="raw_all", align_bytes=1024)
+        res_all = keep.tile([P, M * T // P], F32, name="res_all", align_bytes=1024)
+        used = {"raw": 0, "res": 0}
         raw = {}
         grouped = {}
         codes = {}
@@ -55,9 +58,11 @@ def tile_mix_bilin_fm_silu_kernel(tc, x, wx, c, wc, w_words, w_scales, b, out):
             return slice(g * PASS, (g + 1) * PASS)
 
         def load(name, rows):
-            t = keep.tile([P, PACK, rows.shape[1]], F32, name="raw_" + name, align_bytes=256)
-            nc.sync.dma_start(out=t[:], in_=rows.rearrange("(p i) w -> p i w", i=PACK))
-            raw[name] = t[:]
+            at = used["raw"]
+            used["raw"] = at + PACK * rows.shape[1]
+            t = raw_all[:, at : used["raw"]].rearrange("p (i w) -> p i w", i=PACK)
+            nc.sync.dma_start(out=t, in_=rows.rearrange("(p i) w -> p i w", i=PACK))
+            raw[name] = t
 
         def load_whole(name, rows):
             load(name, rows)
@@ -84,7 +89,7 @@ def tile_mix_bilin_fm_silu_kernel(tc, x, wx, c, wc, w_words, w_scales, b, out):
 
         def load_w_part(n0, n1):
             for a in range(2):
-                t = keep.tile([P, 2 * (n1 - n0) * P], U8, name="w_part%d%d" % (a, n0), align_bytes=256)
+                t = keep.tile([P, 2 * (n1 - n0) * P], U8, name="w_part%d%d" % (a, n0), align_bytes=1024)
                 nc.sync.dma_start(out=t[:].bitcast(I32), in_=w_words[a, :, 2 * n0 * P : 2 * n1 * P].bitcast(I32))
                 for nt in range(n0, n1):
                     w_codes[a, nt] = t[:, 2 * (nt - n0) * P : 2 * (nt - n0 + 1) * P]
@@ -239,7 +244,9 @@ def tile_mix_bilin_fm_silu_kernel(tc, x, wx, c, wc, w_words, w_scales, b, out):
 
         def finish(t0, width, first, group=1, count=None):
             count = count or BANK // width
-            res = keep.tile([P, count, width], F32, name="res%d_%d" % (t0, first), align_bytes=256)
+            at = used["res"]
+            used["res"] = at + count * width
+            res = res_all[:, at : used["res"]].rearrange("p (n t) -> p n t", n=count)
             for i in range(count):
                 nt = first + i
                 nc.scalar.activation(

@@ -108,11 +108,16 @@ def tile_mix_bilin_fm_silu_kernel(tc, x, wx, c, wc, w_words, w_scales, b, out):
             if mv < d.shape[1]:
                 nc.scalar.copy(out=d[:, mv:], in_=s[:, mv:])
 
-        def interleave(name, mv):
+        def interleave(name, mv, end=P):
             g = stage.tile([P, PASS * PACK], BF16, name="grouped", align_bytes=256)
             grouped[name] = g
             order = "p (j m i) -> p m i j" if name[0] == "w" else "p (m j i) -> p m i j"
-            share_copy(g[:].rearrange(order, j=PACK, i=PACK), raw[name].rearrange("p i (m j) -> p m i j", j=PACK), mv)
+            d = g[:].rearrange(order, j=PACK, i=PACK)
+            share_copy(d[:, 0:end], raw[name].rearrange("p i (m j) -> p m i j", j=PACK)[:, 0:end], mv)
+
+        def interleave_rest(name, m0, m1, mv=0):
+            d = grouped[name][:].rearrange("p (j m i) -> p m i j", j=PACK, i=PACK)
+            share_copy(d[:, m0:m1], raw[name].rearrange("p i (m j) -> p m i j", j=PACK)[:, m0:m1], mv)
 
         def interleave_x(name, src, c0, c1, mv):
             g = keep.tile([P, (c1 - c0) * PACK], BF16, name="grouped_" + name, align_bytes=256)
@@ -268,8 +273,8 @@ def tile_mix_bilin_fm_silu_kernel(tc, x, wx, c, wc, w_words, w_scales, b, out):
             nc.scalar.copy(out=bias[:], in_=b_t[:, 0:TILES])
 
         load("c0", c[span(0), :])
-        load_whole("wc0", wc[span(0), :])
         load("c1", c[span(1), :])
+        load_whole("wc0", wc[span(0), :])
         load_whole("wc1", wc[span(1), :])
         load_whole("wx0", wx[span(0), :])
         load("x0", x[span(0), :])
@@ -281,14 +286,14 @@ def tile_mix_bilin_fm_silu_kernel(tc, x, wx, c, wc, w_words, w_scales, b, out):
         load_w_part(3, TILES)
         interleave("c0", 80)
         quant_in("c0")
+        interleave("c1", 80)
+        quant_in("c1")
         interleave("wc00", 80)
         interleave("wc01", 64)
         quant_in("wc00")
         pc_pass(0, 0)
         quant_in("wc01")
         pc_pass(0, 1)
-        interleave("c1", 80)
-        quant_in("c1")
         interleave("wc10", 84)
         quant_in("wc10")
         pc_pass(1, 0)
@@ -298,30 +303,32 @@ def tile_mix_bilin_fm_silu_kernel(tc, x, wx, c, wc, w_words, w_scales, b, out):
         pc_copy(0, (1,))
         pc_copy(1, (), [0, 1])
         interleave("wx00", 128)
+        interleave("wx01", 32, 104)
         quant_in("wx00")
         interleave_x("x0a", "x0", 0, 2 * CH, 64)
-        interleave_x("x0b", "x0", 2 * CH, T, 0)
+        interleave_x("x0b", "x0", 2 * CH, T, 64)
         place_bias()
         quant_x("x0", "x0a", 0, 2 * CH)
         px_pass(0, 0, 0)
         px_pass(0, 0, 1)
-        interleave("wx01", 68)
         quant_x("x0", "x0b", 2 * CH, T)
         px_pass(0, 0, 2)
         px_pass(0, 0, 3)
         interleave_w_pair("wx10", 0, 84)
         interleave_w_pair("wx10", 1, 84)
-        for j in range(PACK):
-            quant_w_tile("wx10", j)
-        pc_copy(1, (), [2])
+        quant_w_tile("wx10", 0)
+        quant_w_tile("wx10", 1)
+        interleave_rest("wx01", 104, P)
         interleave_x("x1a", "x1A", 0, CH, 32)
         interleave_x("x1b", "x1A", CH, 2 * CH, 0)
-        pc_copy(1, (), [3])
+        pc_copy(1, (), [2, 3])
+        quant_w_tile("wx10", 2)
+        quant_w_tile("wx10", 3)
         quant_x("x1", "x1a", 0, CH)
-        quant_x("x1", "x1b", CH, 2 * CH)
         px_pass(1, 0, 0)
-        px_pass(1, 0, 1)
         quant_in("wx01")
+        quant_x("x1", "x1b", CH, 2 * CH)
+        px_pass(1, 0, 1)
         px_pass(0, 1, 0)
         px_pass(0, 1, 1)
         mult(0, 0)

@@ -210,12 +210,13 @@ def tile_mix_bilin_fm_silu_kernel(tc, x, wx, c, wc, w_words, w_scales, b, out):
         h_codes = [keep.tile([P, T], U32, name="h_codes%d" % a, align_bytes=256) for a in range(2)]
         h_scales = [keep.tile([P, T], U8, name="h_scales%d" % a, align_bytes=256) for a in range(2)]
 
-        def mult(a, ch):
-            h[a, ch] = keep.tile([P, CH * PACK], BF16, name="h%d%d" % (a, ch), align_bytes=256)
+        def mult(a, ch, m0=0, m1=CH // 2):
+            if m0 == 0:
+                h[a, ch] = keep.tile([P, CH * PACK], BF16, name="h%d%d" % (a, ch), align_bytes=256)
             nc.vector.tensor_tensor(
-                out=h[a, ch][:].rearrange("p (m i j) -> p m j i", i=2, j=PACK),
-                in0=px_bank[a, ch][:].rearrange("p (j m i) -> p m j i", j=PACK, i=2),
-                in1=pc[a][:, :, ch * CH : (ch + 1) * CH].rearrange("p j (m i) -> p m j i", i=2),
+                out=h[a, ch][:].rearrange("p (m i j) -> p m j i", i=2, j=PACK)[:, m0:m1],
+                in0=px_bank[a, ch][:].rearrange("p (j m i) -> p m j i", j=PACK, i=2)[:, m0:m1],
+                in1=pc[a][:, :, ch * CH : (ch + 1) * CH].rearrange("p j (m i) -> p m j i", i=2)[:, m0:m1],
                 op=mybir.AluOpType.mult,
             )
 
@@ -282,8 +283,8 @@ def tile_mix_bilin_fm_silu_kernel(tc, x, wx, c, wc, w_words, w_scales, b, out):
         load("x1A", x[span(1), 0 : 2 * CH])
         load("wx11", wx[span(1), span(1)])
         load("x1B", x[span(1), 2 * CH : T])
-        load_w_part(0, 3)
-        load_w_part(3, TILES)
+        load_w_part(0, 5)
+        load_w_part(5, TILES)
         interleave("c0", 80)
         quant_in("c0")
         interleave("c1", 80)
@@ -342,56 +343,60 @@ def tile_mix_bilin_fm_silu_kernel(tc, x, wx, c, wc, w_words, w_scales, b, out):
         px_pass(0, 1, 3)
         interleave_x("x1c", "x1B", 0, CH, 0)
         interleave_x("x1d", "x1B", CH, 2 * CH, 0)
+        def y_tile(nt, t0, width, at):
+            y_open((t0, nt), at)
+            cuts = [(c0, min(256, width - c0)) for c0 in range(0, width, 256)]
+            for i, (c0, n) in enumerate(cuts):
+                for a in range(2):
+                    y_mm((t0, nt), c0, a, nt, t0 + c0, n, start=(i == 0 and a == 0), stop=(i == len(cuts) - 1 and a == 1))
+            finish(t0, width, nt, 1, 1)
         mult(0, 1)
         quant_h(0, 0)
-        mult(1, 0)
+        mult(1, 0, 0, 24)
         quant_x("x1", "x1c", 2 * CH, 3 * CH)
-        quant_h(0, 1)
-        mult(1, 1)
-        quant_h(1, 0)
+        mult(1, 0, 24)
         quant_x("x1", "x1d", 3 * CH, T)
+        mult(1, 1)
+        quant_h(0, 1)
+        quant_h(1, 0)
         quant_h(1, 1)
         px_pass(1, 0, 2)
         px_pass(1, 1, 2)
+        px_pass(1, 0, 3)
+        px_pass(1, 1, 3)
         y_open((0, 0), 0)
         y_mm((0, 0), 0, 0, 0, 0, 256, start=True)
-        y_pass(0, 0, 256, 1, 1)
-        y_mm((0, 0), 0, 1, 0, 0, 128)
-        px_pass(1, 0, 3)
-        y_mm((0, 0), 128, 1, 0, 128, 128, stop=True)
+        y_open((0, 1), 1)
+        y_mm((0, 1), 0, 0, 1, 0, 256, start=True)
+        y_mm((0, 0), 0, 1, 0, 0, 256, stop=True)
         finish(0, 256, 0, 1, 1)
-        y_pass(1, 0, 256, 1)
-        finish(0, 256, 1)
-        y_pass(0, 0, 256, 3, 4)
-        y_pass(1, 0, 256, 3)
-        finish(0, 256, 3)
-        px_pass(1, 1, 3)
+        y_mm((0, 1), 0, 1, 1, 0, 256, stop=True)
+        finish(0, 256, 1, 1, 1)
+        y_tile(2, 0, 256, 4)
+        y_tile(3, 0, 256, 5)
         mult(0, 2)
         mult(1, 2)
         quant_h(0, 2)
+        mult(0, 3, 0, 24)
         quant_h(1, 2)
-        mult(0, 3)
+        mult(0, 3, 24)
         mult(1, 3)
         quant_h(0, 3)
         quant_h(1, 3)
-        for nt in range(5, 8):
-            y_open((0, nt), [5, 0, 2][nt - 5])
-            for a in range(2):
-                y_mm((0, nt), 0, a, nt, 0, 256, start=(a == 0))
-            for a in range(2):
-                y_mm((0, nt), 256, a, nt, 256, 128, stop=(a == 1))
-            finish(0, 384, nt)
-        y_pass(0, 256, 256, 0, 1)
-        y_pass(1, 256, 256, 0)
-        finish(256, 256, 0)
-        y_pass(0, 256, 256, 2, 6)
-        y_pass(1, 256, 256, 2)
-        finish(256, 256, 2)
-        y_open((256, 4), 4)
-        y_mm((256, 4), 0, 0, 4, 256, 256, start=True)
-        y_mm((256, 4), 0, 1, 4, 256, 256, stop=True)
-        finish(256, 256, 4, 1, 1)
-        y_open((384, 5), 3)
+        y_tile(4, 0, 256, 2)
+        for nt, at in ((5, 6), (6, 0), (7, 1)):
+            y_tile(nt, 0, 384, at)
+        y_open((256, 0), 4)
+        y_mm((256, 0), 0, 0, 0, 256, 256, start=True)
+        y_open((256, 1), 5)
+        y_mm((256, 1), 0, 0, 1, 256, 256, start=True)
+        y_mm((256, 0), 0, 1, 0, 256, 256, stop=True)
+        finish(256, 256, 0, 1, 1)
+        y_mm((256, 1), 0, 1, 1, 256, 256, stop=True)
+        finish(256, 256, 1, 1, 1)
+        for nt, at in ((2, 2), (3, 3), (4, 7)):
+            y_tile(nt, 256, 256, at)
+        y_open((384, 5), 6)
         for a in range(2):
             for i in range(3):
                 y_mm((384, 5), 128 * i, a, 5 + i, 384, 128, start=(a == 0 and i == 0), stop=(a == 1 and i == 2))

@@ -20,6 +20,7 @@ PACK = 4
 PASS = P * PACK
 CH = 128
 CHUNKS = T // CH
+HALF = T // 2
 TILES = M // P
 BANK = 512
 
@@ -52,156 +53,123 @@ def tile_mix_bilin_fm_silu_kernel(tc, x, wx, c, wc, w_words, w_scales, b, out):
         codes = {}
         scales = {}
         w_codes = {}
-        w_half = {}
 
         def span(g):
             return slice(g * PASS, (g + 1) * PASS)
 
-        def load(name, rows):
+        def load(src, g, c0, c1):
+            name, rows = src
             at = used["raw"]
-            used["raw"] = at + PACK * rows.shape[1]
+            used["raw"] = at + PACK * (c1 - c0)
             t = raw_all[:, at : used["raw"]].rearrange("p (i w) -> p i w", i=PACK)
-            nc.sync.dma_start(out=t, in_=rows.rearrange("(p i) w -> p i w", i=PACK))
-            raw[name] = t
+            nc.sync.dma_start(out=t, in_=rows[span(g), c0:c1].rearrange("(p i) w -> p i w", i=PACK))
+            for col in range(c0, c1, CH):
+                raw[name, g, col] = (t, c0)
 
-        def load_whole(name, rows):
-            load(name, rows)
+        def raw_cols(name, g, c0, c1):
+            t, first = raw[name, g, c0]
+            return t[:, :, c0 - first : c1 - first]
+
+        def load_w(n0, n1):
             for a in range(2):
-                raw[name + str(a)] = raw[name][:, :, span(a)]
-
-        def load_w_scales(n0, n1):
-            w_sc = w_scales[:, :, n0:n1].bitcast(I32)
-            for r in range(4):
-                nc.sync.dma_start(
-                    out=w_plane[r:P:32, :, n0:n1].bitcast(I32),
-                    in_=w_sc[:, r:16:4, :].rearrange("a q n -> q a n"),
-                )
-
-        def load_w_codes(a):
-            w_codes[a] = keep.tile([P, 2 * M], U8, name="w_codes%d" % a, align_bytes=256)
-            nc.sync.dma_start(out=w_codes[a][:].bitcast(I32), in_=w_words[a].bitcast(I32))
-
-        def load_w_all():
-            t = keep.tile([P, 2, 2 * M], U8, name="w_codes", align_bytes=256)
-            nc.sync.dma_start(out=t[:].bitcast(I32), in_=w_words.bitcast(I32).rearrange("a p n -> p a n"))
-            for a in range(2):
-                w_codes[a] = t[:, a, :]
-
-        def load_w_part(n0, n1):
-            for a in range(2):
-                t = keep.tile([P, 2 * (n1 - n0) * P], U8, name="w_part%d%d" % (a, n0), align_bytes=1024)
+                t = keep.tile([P, 2 * (n1 - n0) * P], U8, name="w_part%d%d" % (a, n0), align_bytes=256)
                 nc.sync.dma_start(out=t[:].bitcast(I32), in_=w_words[a, :, 2 * n0 * P : 2 * n1 * P].bitcast(I32))
                 for nt in range(n0, n1):
                     w_codes[a, nt] = t[:, 2 * (nt - n0) * P : 2 * (nt - n0 + 1) * P]
-            load_w_scales(n0 * P, n1 * P)
+            w_sc = w_scales[:, :, n0 * P : n1 * P].bitcast(I32)
+            for r in range(4):
+                nc.sync.dma_start(
+                    out=w_plane[r:P:32, :, n0 * P : n1 * P].bitcast(I32),
+                    in_=w_sc[:, r:16:4, :].rearrange("a q n -> q a n"),
+                )
 
-        def w_tile(a, nt):
-            return w_codes[a, nt]
+        def copy_on(engine, d, s):
+            if engine == "V":
+                nc.vector.tensor_copy(out=d, in_=s)
+            else:
+                nc.scalar.copy(out=d, in_=s)
 
-        def load_bias():
-            with nc.allow_non_contiguous_dma(reason="one bias value for each partition and output tile"):
-                nc.sync.dma_start(out=bias[:], in_=b.rearrange("(i p) -> p i", p=P))
+        def round_w(name, g, a, engine, m0, m1):
+            key = (name, g, a)
+            if key not in grouped:
+                grouped[key] = stage.tile([P, PASS * PACK], BF16, name="grouped", align_bytes=256)
+            d = grouped[key][:].rearrange("p (j m i) -> p m i j", j=PACK, i=PACK)
+            s = raw_cols(name, g, a * PASS, (a + 1) * PASS).rearrange("p i (m j) -> p m i j", j=PACK)
+            copy_on(engine, d[:, m0:m1], s[:, m0:m1])
 
-        def share_copy(d, s, mv):
-            if mv > 0:
-                nc.vector.tensor_copy(out=d[:, 0:mv], in_=s[:, 0:mv])
-            if mv < d.shape[1]:
-                nc.scalar.copy(out=d[:, mv:], in_=s[:, mv:])
+        def round_w_pair(name, g, a, u, engine, m0, m1):
+            key = (name, g, a, u)
+            if key not in grouped:
+                grouped[key] = keep.tile([P, 2 * PASS], BF16, name="grouped_%s%d%d%d" % key, align_bytes=64)
+            d = grouped[key][:].rearrange("p (e m i) -> p m i e", e=2, i=PACK)
+            s = raw_cols(name, g, a * PASS, (a + 1) * PASS).rearrange("p i (m u e) -> p u m i e", u=2, e=2)[:, u]
+            copy_on(engine, d[:, m0:m1], s[:, m0:m1])
 
-        def interleave(name, mv, end=P):
-            g = stage.tile([P, PASS * PACK], BF16, name="grouped", align_bytes=256)
-            grouped[name] = g
-            order = "p (j m i) -> p m i j" if name[0] == "w" else "p (m j i) -> p m i j"
-            d = g[:].rearrange(order, j=PACK, i=PACK)
-            share_copy(d[:, 0:end], raw[name].rearrange("p i (m j) -> p m i j", j=PACK)[:, 0:end], mv)
+        def round_act(name, g, t0, t1, engine, m0, m1):
+            key = (name, g, t0)
+            if key not in grouped:
+                if t1 - t0 == T:
+                    grouped[key] = stage.tile([P, PASS * PACK], BF16, name="grouped", align_bytes=256)
+                else:
+                    grouped[key] = keep.tile([P, (t1 - t0) * PACK], BF16, name="grouped_%s%d%d" % key, align_bytes=64)
+            d = grouped[key][:].rearrange("p (m j i) -> p m i j", j=PACK, i=PACK)
+            s = raw_cols(name, g, t0, t1).rearrange("p i (m j) -> p m i j", j=PACK)
+            copy_on(engine, d[:, m0:m1], s[:, m0:m1])
 
-        def interleave_rest(name, m0, m1, mv=0):
-            d = grouped[name][:].rearrange("p (j m i) -> p m i j", j=PACK, i=PACK)
-            share_copy(d[:, m0:m1], raw[name].rearrange("p i (m j) -> p m i j", j=PACK)[:, m0:m1], mv)
+        def quant_into(key, src, c0, c1):
+            if key not in codes:
+                label = "".join(str(part) for part in key)
+                codes[key] = keep.tile([P, PASS], U32, name="codes_" + label, align_bytes=256)
+                scales[key] = keep.tile([P, PASS], U8, name="scales_" + label, align_bytes=256)
+            fmt = E5M2 if key[0] == "c" else E4M3
+            nc.vector.quantize_mx(out=codes[key][:, c0:c1].bitcast(fmt), scales=scales[key][:, c0:c1], in_=src)
 
-        def interleave_x(name, src, c0, c1, mv):
-            g = keep.tile([P, (c1 - c0) * PACK], BF16, name="grouped_" + name, align_bytes=256)
-            grouped[name] = g
-            s = raw[src][:, :, c0:c1].rearrange("p i (m j) -> p m i j", j=PACK)
-            share_copy(g[:].rearrange("p (m j i) -> p m i j", j=PACK, i=PACK), s, mv)
+        def quant_w(name, g, a, j0=0, j1=PACK):
+            quant_into((name, g, a), grouped[name, g, a][:, j0 * PASS : j1 * PASS], j0 * P, j1 * P)
 
-        def interleave_w_pair(name, u, mv):
-            g = keep.tile([P, 2 * P * PACK], BF16, name="grouped_%s%d" % (name, u), align_bytes=256)
-            grouped[name, u] = g
-            s = raw[name].rearrange("p i (m u e) -> p u m i e", u=2, e=2)[:, u]
-            share_copy(g[:].rearrange("p (e m i) -> p m i e", e=2, i=PACK), s, mv)
+        def quant_w_pair(name, g, a, u, e0=0, e1=2):
+            quant_into((name, g, a), grouped[name, g, a, u][:, e0 * PASS : e1 * PASS], (2 * u + e0) * P, (2 * u + e1) * P)
 
-        def interleave_w_half(name, mv):
-            g = keep.tile([P, PASS * PACK // 2], BF16, name="grouped_" + name, align_bytes=256)
-            grouped[name] = g
-            s = raw[name].rearrange("p i (m j) -> p m i j", j=PACK)
-            share_copy(g[:].rearrange("p (j m i) -> p m i j", j=PACK, i=PACK), s, mv)
-
-        def quant_w_half(dst, name, u, j):
-            half = P // 2
-            quant_into(dst, grouped[name][:, j * half * PACK : (j + 1) * half * PACK], slice(j * P + u * half, j * P + (u + 1) * half))
-
-        def quant_into(name, src, cols):
-            if name not in codes:
-                codes[name] = keep.tile([P, PASS], U32, name="codes_" + name, align_bytes=256)
-                scales[name] = keep.tile([P, PASS], U8, name="scales_" + name, align_bytes=256)
-            fmt = E5M2 if name[0] == "c" else E4M3
-            nc.vector.quantize_mx(out=codes[name][:, cols].bitcast(fmt), scales=scales[name][:, cols], in_=src)
-
-        def quant_in(name):
-            quant_into(name, grouped[name][:], slice(0, PASS))
-
-        def quant_x(dst, name, t0, t1):
-            quant_into(dst, grouped[name][:], slice(t0, t1))
-
-        def quant_w_tile(name, j):
-            quant_into(name, grouped[name, j // 2][:, (j % 2) * PASS : (j % 2 + 1) * PASS], slice(j * P, (j + 1) * P))
+        def quant_act(name, g, t0, t1):
+            quant_into((name, g), grouped[name, g, t0][:], t0, t1)
 
         pc_bank = {}
         pc = {}
 
-        def pc_pass(g, a):
-            wname = "wc%d%d" % (g, a)
-            cname = "c%d" % g
-            for j in range(PACK):
+        def pc_pass(g, a, tiles=range(PACK)):
+            for j in tiles:
                 if g == 0:
                     pc_bank[a, j] = bank(PACK * a + j)
                 cols = slice(j * P, (j + 1) * P)
                 nc.tensor.matmul_mx(
                     out=pc_bank[a, j][:],
-                    lhsT=codes[wname][:, cols].bitcast(E4M3),
-                    lhsT_scale=scales[wname][:, cols],
-                    rhs=codes[cname][:].bitcast(E5M2),
-                    rhs_scale=scales[cname][:],
+                    lhsT=codes["wc", g, a][:, cols].bitcast(E4M3),
+                    lhsT_scale=scales["wc", g, a][:, cols],
+                    rhs=codes["c", g][:].bitcast(E5M2),
+                    rhs_scale=scales["c", g][:],
                     start=(g == 0),
                     stop=(g == 1),
                 )
 
-        def pc_copy(a, on_vector, tiles=range(PACK)):
+        def pc_copy(a, j, engine):
             if a not in pc:
                 pc[a] = keep.tile([P, PACK, T], F32, name="pc%d" % a)
-            for j in tiles:
-                if j in on_vector:
-                    nc.vector.tensor_copy(out=pc[a][:, j, :], in_=pc_bank[a, j][:])
-                else:
-                    nc.scalar.copy(out=pc[a][:, j, :], in_=pc_bank[a, j][:])
+            copy_on(engine, pc[a][:, j, :], pc_bank[a, j][:])
 
         px_bank = {}
 
         def px_pass(g, a, ch, tiles=range(PACK), at=None):
-            wname = "wx%d%d" % (g, a)
-            xname = "x%d" % g
-            if g == 0:
+            if (a, ch) not in px_bank:
                 px_bank[a, ch] = bank(CHUNKS * a + ch if at is None else at)
             tcols = slice(ch * CH, (ch + 1) * CH)
             for j in tiles:
                 cols = slice(j * P, (j + 1) * P)
                 nc.tensor.matmul_mx(
                     out=px_bank[a, ch][:, j * CH : (j + 1) * CH],
-                    lhsT=codes[wname][:, cols].bitcast(E4M3),
-                    lhsT_scale=scales[wname][:, cols],
-                    rhs=codes[xname][:, tcols].bitcast(E4M3),
-                    rhs_scale=scales[xname][:, tcols],
+                    lhsT=codes["wx", g, a][:, cols].bitcast(E4M3),
+                    lhsT_scale=scales["wx", g, a][:, cols],
+                    rhs=codes["x", g][:, tcols].bitcast(E4M3),
+                    rhs_scale=scales["x", g][:, tcols],
                     start=(g == 0 and j == 0),
                     stop=(g == 1 and j == PACK - 1),
                 )
@@ -212,7 +180,7 @@ def tile_mix_bilin_fm_silu_kernel(tc, x, wx, c, wc, w_words, w_scales, b, out):
 
         def mult(a, ch, m0=0, m1=CH // 2):
             if m0 == 0:
-                h[a, ch] = keep.tile([P, CH * PACK], BF16, name="h%d%d" % (a, ch), align_bytes=256)
+                h[a, ch] = keep.tile([P, CH * PACK], BF16, name="h%d%d" % (a, ch), align_bytes=64)
             nc.vector.tensor_tensor(
                 out=h[a, ch][:].rearrange("p (m i j) -> p m j i", i=2, j=PACK)[:, m0:m1],
                 in0=px_bank[a, ch][:].rearrange("p (j m i) -> p m j i", j=PACK, i=2)[:, m0:m1],
@@ -226,14 +194,11 @@ def tile_mix_bilin_fm_silu_kernel(tc, x, wx, c, wc, w_words, w_scales, b, out):
 
         y_bank = {}
 
-        def y_open(key, at):
-            y_bank[key] = bank(at)
-
         def y_mm(key, col, a, nt, t0, width, start=False, stop=False):
             cols = slice(t0, t0 + width)
             nc.tensor.matmul_mx(
                 out=y_bank[key][:, col : col + width],
-                lhsT=w_tile(a, nt).bitcast(E2M1),
+                lhsT=w_codes[a, nt].bitcast(E2M1),
                 lhsT_scale=w_plane[:, a, nt * P : (nt + 1) * P],
                 rhs=h_codes[a][:, cols].bitcast(E4M3),
                 rhs_scale=h_scales[a][:, cols],
@@ -241,121 +206,141 @@ def tile_mix_bilin_fm_silu_kernel(tc, x, wx, c, wc, w_words, w_scales, b, out):
                 stop=stop,
             )
 
-        def y_pass(a, t0, width, first, at=None):
-            count = BANK // width
-            if a == 0:
-                y_open((t0, first), at)
-            for i in range(count):
-                y_mm((t0, first), i * width, a, first + i, t0, width, a == 0 and i == 0, a == 1 and i == count - 1)
-
-        def finish(t0, width, first, group=1, count=None):
-            count = count or BANK // width
+        def finish(key, col, nt, t0, width):
             at = used["res"]
-            used["res"] = at + count * width
-            res = res_all[:, at : used["res"]].rearrange("p (n t) -> p n t", n=count)
-            for i in range(count):
-                nt = first + i
-                nc.scalar.activation(
-                    out=res[:, i, :],
-                    in_=y_bank[t0, first][:, i * width : (i + 1) * width],
-                    func=mybir.ActivationFunctionType.Silu,
-                    bias=bias[:, nt : nt + 1],
-                )
-                if (i + 1) % group == 0:
-                    n0 = nt + 1 - group
-                    nc.sync.dma_start(
-                        out=out[n0 * P : (nt + 1) * P, t0 : t0 + width].rearrange("(n p) t -> p n t", p=P),
-                        in_=res[:, i + 1 - group : i + 1, :],
-                    )
+            used["res"] = at + width
+            res = res_all[:, at : at + width]
+            nc.scalar.activation(
+                out=res,
+                in_=y_bank[key][:, col : col + width],
+                func=mybir.ActivationFunctionType.Silu,
+                bias=bias[:, nt : nt + 1],
+            )
+            nc.sync.dma_start(out=out[nt * P : (nt + 1) * P, t0 : t0 + width], in_=res)
 
-        def place_bias():
-            b_t = bank(5)
+        def y_first(nt, t0, width, at):
+            y_bank[t0, nt] = bank(at)
+            y_mm((t0, nt), 0, 0, nt, t0, width, start=True)
+
+        def y_second(nt, t0, width):
+            y_mm((t0, nt), 0, 1, nt, t0, width, stop=True)
+            finish((t0, nt), 0, nt, t0, width)
+
+        def y_tile(nt, t0, width, at):
+            y_bank[t0, nt] = bank(at)
+            cuts = [(0, width)] if width != 3 * CH else [(0, HALF), (HALF, CH)]
+            for i, (c0, n) in enumerate(cuts):
+                for a in range(2):
+                    y_mm((t0, nt), c0, a, nt, t0 + c0, n, start=(i == 0 and a == 0), stop=(i == len(cuts) - 1 and a == 1))
+            finish((t0, nt), 0, nt, t0, width)
+
+        def y_short(tiles, t0, at):
+            key = (t0, tiles[0])
+            y_bank[key] = bank(at)
+            for a in range(2):
+                for i, nt in enumerate(tiles):
+                    y_mm(key, CH * i, a, nt, t0, CH, start=(a == 0 and i == 0), stop=(a == 1 and i == len(tiles) - 1))
+            for i, nt in enumerate(tiles):
+                finish(key, CH * i, nt, t0, CH)
+
+        def place_bias(at):
+            b_t = bank(at)
             nc.tensor.transpose(b_t[:, 0:P], b_rows[:], ident[:])
             nc.scalar.copy(out=bias[:], in_=b_t[:, 0:TILES])
 
-        load("c0", c[span(0), :])
-        load("c1", c[span(1), :])
-        load_whole("wc0", wc[span(0), :])
-        load_whole("wc1", wc[span(1), :])
-        load_whole("wx0", wx[span(0), :])
-        load("x0", x[span(0), :])
-        load("wx10", wx[span(1), span(0)])
-        load("x1A", x[span(1), 0 : 2 * CH])
-        load("wx11", wx[span(1), span(1)])
-        load("x1B", x[span(1), 2 * CH : T])
-        load_w_part(0, 5)
-        load_w_part(5, TILES)
-        interleave("c0", 80)
-        quant_in("c0")
-        interleave("c1", 80)
-        quant_in("c1")
-        interleave("wc00", 80)
-        interleave("wc01", 64)
-        quant_in("wc00")
+        X, C, WX, WC = ("x", x), ("c", c), ("wx", wx), ("wc", wc)
+
+        load(C, 0, 0, T)
+        load(C, 1, 0, T)
+        load(WC, 0, 0, R)
+        load(WC, 1, 0, R)
+        load(WX, 0, 0, R)
+        load(X, 0, 0, T)
+        load(WX, 1, 0, PASS)
+        load(X, 1, 0, HALF)
+        load(WX, 1, PASS, R)
+        load(X, 1, HALF, T)
+        load_w(0, 5)
+        load_w(5, TILES)
+
+        for g in range(2):
+            round_act("c", g, 0, T, "V", 0, 80)
+            round_act("c", g, 0, T, "S", 80, P)
+            quant_act("c", g, 0, T)
+        round_w("wc", 0, 0, "V", 0, 80)
+        round_w("wc", 0, 0, "S", 80, P)
+        round_w("wc", 0, 1, "V", 0, 64)
+        round_w("wc", 0, 1, "S", 64, P)
+        quant_w("wc", 0, 0)
         pc_pass(0, 0)
-        quant_in("wc01")
+        quant_w("wc", 0, 1)
         pc_pass(0, 1)
-        interleave("wc10", 84)
-        quant_in("wc10")
+        round_w("wc", 1, 0, "V", 0, 84)
+        round_w("wc", 1, 0, "S", 84, P)
+        quant_w("wc", 1, 0)
         pc_pass(1, 0)
-        interleave("wc11", 64)
-        quant_in("wc11")
+        round_w("wc", 1, 1, "V", 0, 64)
+        round_w("wc", 1, 1, "S", 64, P)
+        quant_w("wc", 1, 1)
         pc_pass(1, 1)
-        pc_copy(0, (1,))
-        pc_copy(1, (), [0, 1])
-        interleave("wx00", 128)
-        interleave("wx01", 32, 104)
-        quant_in("wx00")
-        interleave_x("x0a", "x0", 0, 2 * CH, 64)
-        interleave_x("x0b", "x0", 2 * CH, T, 64)
-        place_bias()
-        quant_x("x0", "x0a", 0, 2 * CH)
+
+        pc_copy(0, 0, "S")
+        pc_copy(0, 1, "V")
+        pc_copy(0, 2, "S")
+        pc_copy(0, 3, "S")
+        pc_copy(1, 0, "S")
+        pc_copy(1, 1, "S")
+        round_w("wx", 0, 0, "V", 0, P)
+        round_w("wx", 0, 1, "V", 0, 32)
+        round_w("wx", 0, 1, "S", 32, 104)
+        quant_w("wx", 0, 0)
+        round_act("x", 0, 0, HALF, "V", 0, 64)
+        round_act("x", 0, HALF, T, "V", 0, 64)
+        place_bias(5)
+        quant_act("x", 0, 0, HALF)
         px_pass(0, 0, 0)
         px_pass(0, 0, 1)
-        quant_x("x0", "x0b", 2 * CH, T)
+        quant_act("x", 0, HALF, T)
         px_pass(0, 0, 2)
         px_pass(0, 0, 3)
-        interleave_w_pair("wx10", 0, 84)
-        interleave_w_pair("wx10", 1, 84)
-        quant_w_tile("wx10", 0)
-        quant_w_tile("wx10", 1)
-        interleave_rest("wx01", 104, P)
-        interleave_x("x1a", "x1A", 0, CH, 32)
-        interleave_x("x1b", "x1A", CH, 2 * CH, 0)
-        pc_copy(1, (), [2, 3])
-        quant_w_tile("wx10", 2)
-        quant_w_tile("wx10", 3)
-        quant_x("x1", "x1a", 0, CH)
+        for u in range(2):
+            round_w_pair("wx", 1, 0, u, "V", 0, 84)
+            round_w_pair("wx", 1, 0, u, "S", 84, P)
+        quant_w_pair("wx", 1, 0, 0, 0, 1)
+        quant_w_pair("wx", 1, 0, 0, 1, 2)
+        round_w("wx", 0, 1, "S", 104, P)
+        round_act("x", 1, 0, CH, "V", 0, 32)
+        round_act("x", 1, CH, HALF, "S", 0, 32)
+        pc_copy(1, 2, "S")
+        pc_copy(1, 3, "S")
+        quant_w_pair("wx", 1, 0, 1, 0, 1)
+        quant_w_pair("wx", 1, 0, 1, 1, 2)
+        quant_act("x", 1, 0, CH)
         px_pass(1, 0, 0)
-        quant_in("wx01")
-        quant_x("x1", "x1b", CH, 2 * CH)
+        quant_w("wx", 0, 1)
+        quant_act("x", 1, CH, HALF)
         px_pass(1, 0, 1)
         px_pass(0, 1, 0)
         px_pass(0, 1, 1)
         mult(0, 0)
         px_pass(0, 1, 2)
-        interleave_w_pair("wx11", 0, 84)
-        interleave_w_pair("wx11", 1, 84)
+        for u in range(2):
+            round_w_pair("wx", 1, 1, u, "V", 0, 84)
+            round_w_pair("wx", 1, 1, u, "S", 84, P)
         for j in range(PACK):
-            quant_w_tile("wx11", j)
+            quant_w_pair("wx", 1, 1, j // 2, j % 2, j % 2 + 1)
             px_pass(1, 1, 0, [j])
         px_pass(1, 1, 1)
         px_pass(0, 1, 3)
-        interleave_x("x1c", "x1B", 0, CH, 0)
-        interleave_x("x1d", "x1B", CH, 2 * CH, 0)
-        def y_tile(nt, t0, width, at):
-            y_open((t0, nt), at)
-            cuts = [(c0, min(256, width - c0)) for c0 in range(0, width, 256)]
-            for i, (c0, n) in enumerate(cuts):
-                for a in range(2):
-                    y_mm((t0, nt), c0, a, nt, t0 + c0, n, start=(i == 0 and a == 0), stop=(i == len(cuts) - 1 and a == 1))
-            finish(t0, width, nt, 1, 1)
+        round_act("x", 1, HALF, 3 * CH, "S", 0, 32)
+        round_act("x", 1, 3 * CH, T, "S", 0, 32)
+
         mult(0, 1)
         quant_h(0, 0)
         mult(1, 0, 0, 24)
-        quant_x("x1", "x1c", 2 * CH, 3 * CH)
+        quant_act("x", 1, HALF, 3 * CH)
         mult(1, 0, 24)
-        quant_x("x1", "x1d", 3 * CH, T)
+        quant_act("x", 1, 3 * CH, T)
         mult(1, 1)
         quant_h(0, 1)
         quant_h(1, 0)
@@ -364,16 +349,12 @@ def tile_mix_bilin_fm_silu_kernel(tc, x, wx, c, wc, w_words, w_scales, b, out):
         px_pass(1, 1, 2)
         px_pass(1, 0, 3)
         px_pass(1, 1, 3)
-        y_open((0, 0), 0)
-        y_mm((0, 0), 0, 0, 0, 0, 256, start=True)
-        y_open((0, 1), 1)
-        y_mm((0, 1), 0, 0, 1, 0, 256, start=True)
-        y_mm((0, 0), 0, 1, 0, 0, 256, stop=True)
-        finish(0, 256, 0, 1, 1)
-        y_mm((0, 1), 0, 1, 1, 0, 256, stop=True)
-        finish(0, 256, 1, 1, 1)
-        y_tile(2, 0, 256, 4)
-        y_tile(3, 0, 256, 5)
+        y_first(0, 0, HALF, 0)
+        y_first(1, 0, HALF, 1)
+        y_second(0, 0, HALF)
+        y_second(1, 0, HALF)
+        y_tile(2, 0, HALF, 4)
+        y_tile(3, 0, HALF, 5)
         mult(0, 2)
         mult(1, 2)
         quant_h(0, 2)
@@ -383,21 +364,13 @@ def tile_mix_bilin_fm_silu_kernel(tc, x, wx, c, wc, w_words, w_scales, b, out):
         mult(1, 3)
         quant_h(0, 3)
         quant_h(1, 3)
-        y_tile(4, 0, 256, 2)
+        y_tile(4, 0, HALF, 2)
         for nt, at in ((5, 6), (6, 0), (7, 1)):
-            y_tile(nt, 0, 384, at)
-        y_open((256, 0), 4)
-        y_mm((256, 0), 0, 0, 0, 256, 256, start=True)
-        y_open((256, 1), 5)
-        y_mm((256, 1), 0, 0, 1, 256, 256, start=True)
-        y_mm((256, 0), 0, 1, 0, 256, 256, stop=True)
-        finish(256, 256, 0, 1, 1)
-        y_mm((256, 1), 0, 1, 1, 256, 256, stop=True)
-        finish(256, 256, 1, 1, 1)
+            y_tile(nt, 0, 3 * CH, at)
+        y_first(0, HALF, HALF, 4)
+        y_first(1, HALF, HALF, 5)
+        y_second(0, HALF, HALF)
+        y_second(1, HALF, HALF)
         for nt, at in ((2, 2), (3, 3), (4, 7)):
-            y_tile(nt, 256, 256, at)
-        y_open((384, 5), 6)
-        for a in range(2):
-            for i in range(3):
-                y_mm((384, 5), 128 * i, a, 5 + i, 384, 128, start=(a == 0 and i == 0), stop=(a == 1 and i == 2))
-        finish(384, 128, 5, 1, 3)
+            y_tile(nt, HALF, HALF, at)
+        y_short((5, 6, 7), 3 * CH, 6)

from contextlib import ExitStack

import concourse.mybir as mybir
from concourse.masks import make_identity

K, R, M, T = 1024, 1024, 1024, 512
FLOPS = 2 * (K * R * T + K * R * T + R * M * T)

F32 = mybir.dt.float32
BF16 = mybir.dt.bfloat16
U32 = mybir.dt.uint32
I32 = mybir.dt.int32
U8 = mybir.dt.uint8
E4M3 = mybir.dt.float8_e4m3fn_x4
E5M2 = mybir.dt.float8_e5m2_x4
E2M1 = mybir.dt.float4_e2m1fn_x4

P = 128
PACK = 4
PASS = P * PACK
CH = 128
CHUNKS = T // CH
HALF = T // 2
TILES = M // P
BANK = 512


def tile_mix_bilin_fm_silu_kernel(tc, x, wx, c, wc, w_words, w_scales, b, out):
    nc = tc.nc
    with ExitStack() as ctx:
        keep = ctx.enter_context(tc.tile_pool(name="keep", bufs=1))
        stage = ctx.enter_context(tc.tile_pool(name="stage", bufs=6))
        psum = ctx.enter_context(tc.psum_pool(name="psum", bufs=1))
        ctx.enter_context(tc.manual_schedule())

        def bank(i):
            return psum.tile([P, BANK], F32, name="bank%d" % i)

        b_rows = keep.tile([P, P], F32, name="b_rows")
        ident = keep.tile([P, P], F32, name="ident")
        w_plane = keep.tile([P, 2, M], U8, name="w_plane", align_bytes=1024)
        bias = keep.tile([P, TILES], F32, name="bias")
        nc.gpsimd.memset(b_rows[:], 0.0)
        nc.gpsimd.memset(w_plane[:].rearrange("p a n -> p (a n)").bitcast(I32), 0)
        make_identity(nc, ident[:])
        nc.scalar.dma_start(out=b_rows[0:TILES, :], in_=b.rearrange("(i p) -> i p", p=P))

        raw_all = keep.tile([P, 2 * (R + T) * K // P], F32, name="raw_all", align_bytes=1024)
        res_all = keep.tile([P, M * T // P], F32, name="res_all", align_bytes=1024)
        used = {"raw": 0, "res": 0}
        raw = {}
        grouped = {}
        codes = {}
        scales = {}
        w_codes = {}

        def span(g):
            return slice(g * PASS, (g + 1) * PASS)

        def load(src, g, c0, c1):
            name, rows = src
            at = used["raw"]
            used["raw"] = at + PACK * (c1 - c0)
            t = raw_all[:, at : used["raw"]].rearrange("p (i w) -> p i w", i=PACK)
            nc.sync.dma_start(out=t, in_=rows[span(g), c0:c1].rearrange("(p i) w -> p i w", i=PACK))
            for col in range(c0, c1, CH):
                raw[name, g, col] = (t, c0)

        def raw_cols(name, g, c0, c1):
            t, first = raw[name, g, c0]
            return t[:, :, c0 - first : c1 - first]

        def load_w(n0, n1):
            for a in range(2):
                t = keep.tile([P, 2 * (n1 - n0) * P], U8, name="w_part%d%d" % (a, n0), align_bytes=256)
                nc.sync.dma_start(out=t[:].bitcast(I32), in_=w_words[a, :, 2 * n0 * P : 2 * n1 * P].bitcast(I32))
                for nt in range(n0, n1):
                    w_codes[a, nt] = t[:, 2 * (nt - n0) * P : 2 * (nt - n0 + 1) * P]
            w_sc = w_scales[:, :, n0 * P : n1 * P].bitcast(I32)
            for r in range(4):
                nc.sync.dma_start(
                    out=w_plane[r:P:32, :, n0 * P : n1 * P].bitcast(I32),
                    in_=w_sc[:, r:16:4, :].rearrange("a q n -> q a n"),
                )

        def copy_on(engine, d, s):
            if engine == "V":
                nc.vector.tensor_copy(out=d, in_=s)
            else:
                nc.scalar.copy(out=d, in_=s)

        def round_w(name, g, a, engine, m0, m1):
            key = (name, g, a)
            if key not in grouped:
                grouped[key] = stage.tile([P, PASS * PACK], BF16, name="grouped", align_bytes=256)
            d = grouped[key][:].rearrange("p (j m i) -> p m i j", j=PACK, i=PACK)
            s = raw_cols(name, g, a * PASS, (a + 1) * PASS).rearrange("p i (m j) -> p m i j", j=PACK)
            copy_on(engine, d[:, m0:m1], s[:, m0:m1])

        def round_w_pair(name, g, a, u, engine, m0, m1):
            key = (name, g, a, u)
            if key not in grouped:
                grouped[key] = keep.tile([P, 2 * PASS], BF16, name="grouped_%s%d%d%d" % key, align_bytes=64)
            d = grouped[key][:].rearrange("p (e m i) -> p m i e", e=2, i=PACK)
            s = raw_cols(name, g, a * PASS, (a + 1) * PASS).rearrange("p i (m u e) -> p u m i e", u=2, e=2)[:, u]
            copy_on(engine, d[:, m0:m1], s[:, m0:m1])

        def round_act(name, g, t0, t1, engine, m0, m1):
            key = (name, g, t0)
            if key not in grouped:
                if t1 - t0 == T:
                    grouped[key] = stage.tile([P, PASS * PACK], BF16, name="grouped", align_bytes=256)
                else:
                    grouped[key] = keep.tile([P, (t1 - t0) * PACK], BF16, name="grouped_%s%d%d" % key, align_bytes=64)
            d = grouped[key][:].rearrange("p (m j i) -> p m i j", j=PACK, i=PACK)
            s = raw_cols(name, g, t0, t1).rearrange("p i (m j) -> p m i j", j=PACK)
            copy_on(engine, d[:, m0:m1], s[:, m0:m1])

        def quant_into(key, src, c0, c1):
            if key not in codes:
                label = "".join(str(part) for part in key)
                codes[key] = keep.tile([P, PASS], U32, name="codes_" + label, align_bytes=256)
                scales[key] = keep.tile([P, PASS], U8, name="scales_" + label, align_bytes=256)
            fmt = E5M2 if key[0] == "c" else E4M3
            nc.vector.quantize_mx(out=codes[key][:, c0:c1].bitcast(fmt), scales=scales[key][:, c0:c1], in_=src)

        def quant_w(name, g, a, j0=0, j1=PACK):
            quant_into((name, g, a), grouped[name, g, a][:, j0 * PASS : j1 * PASS], j0 * P, j1 * P)

        def quant_w_pair(name, g, a, u, e0=0, e1=2):
            quant_into((name, g, a), grouped[name, g, a, u][:, e0 * PASS : e1 * PASS], (2 * u + e0) * P, (2 * u + e1) * P)

        def quant_act(name, g, t0, t1):
            quant_into((name, g), grouped[name, g, t0][:], t0, t1)

        pc_bank = {}
        pc = {}

        def pc_pass(g, a, tiles=range(PACK)):
            for j in tiles:
                if g == 0:
                    pc_bank[a, j] = bank(PACK * a + j)
                cols = slice(j * P, (j + 1) * P)
                nc.tensor.matmul_mx(
                    out=pc_bank[a, j][:],
                    lhsT=codes["wc", g, a][:, cols].bitcast(E4M3),
                    lhsT_scale=scales["wc", g, a][:, cols],
                    rhs=codes["c", g][:].bitcast(E5M2),
                    rhs_scale=scales["c", g][:],
                    start=(g == 0),
                    stop=(g == 1),
                )

        def pc_copy(a, j, engine):
            if a not in pc:
                pc[a] = keep.tile([P, PACK, T], F32, name="pc%d" % a)
            copy_on(engine, pc[a][:, j, :], pc_bank[a, j][:])

        px_bank = {}

        def px_pass(g, a, ch, tiles=range(PACK), at=None):
            if (a, ch) not in px_bank:
                px_bank[a, ch] = bank(CHUNKS * a + ch if at is None else at)
            tcols = slice(ch * CH, (ch + 1) * CH)
            for j in tiles:
                cols = slice(j * P, (j + 1) * P)
                nc.tensor.matmul_mx(
                    out=px_bank[a, ch][:, j * CH : (j + 1) * CH],
                    lhsT=codes["wx", g, a][:, cols].bitcast(E4M3),
                    lhsT_scale=scales["wx", g, a][:, cols],
                    rhs=codes["x", g][:, tcols].bitcast(E4M3),
                    rhs_scale=scales["x", g][:, tcols],
                    start=(g == 0 and j == 0),
                    stop=(g == 1 and j == PACK - 1),
                )

        h = {}
        h_codes = [keep.tile([P, T], U32, name="h_codes%d" % a, align_bytes=256) for a in range(2)]
        h_scales = [keep.tile([P, T], U8, name="h_scales%d" % a, align_bytes=256) for a in range(2)]

        def mult(a, ch, m0=0, m1=CH // 2):
            if m0 == 0:
                h[a, ch] = keep.tile([P, CH * PACK], BF16, name="h%d%d" % (a, ch), align_bytes=64)
            nc.vector.tensor_tensor(
                out=h[a, ch][:].rearrange("p (m i j) -> p m j i", i=2, j=PACK)[:, m0:m1],
                in0=px_bank[a, ch][:].rearrange("p (j m i) -> p m j i", j=PACK, i=2)[:, m0:m1],
                in1=pc[a][:, :, ch * CH : (ch + 1) * CH].rearrange("p j (m i) -> p m j i", i=2)[:, m0:m1],
                op=mybir.AluOpType.mult,
            )

        def quant_h(a, ch):
            cols = slice(ch * CH, (ch + 1) * CH)
            nc.vector.quantize_mx(out=h_codes[a][:, cols].bitcast(E4M3), scales=h_scales[a][:, cols], in_=h[a, ch][:])

        y_bank = {}

        def y_mm(key, col, a, nt, t0, width, start=False, stop=False):
            cols = slice(t0, t0 + width)
            nc.tensor.matmul_mx(
                out=y_bank[key][:, col : col + width],
                lhsT=w_codes[a, nt].bitcast(E2M1),
                lhsT_scale=w_plane[:, a, nt * P : (nt + 1) * P],
                rhs=h_codes[a][:, cols].bitcast(E4M3),
                rhs_scale=h_scales[a][:, cols],
                start=start,
                stop=stop,
            )

        def finish(key, col, nt, t0, width):
            at = used["res"]
            used["res"] = at + width
            res = res_all[:, at : at + width]
            nc.scalar.activation(
                out=res,
                in_=y_bank[key][:, col : col + width],
                func=mybir.ActivationFunctionType.Silu,
                bias=bias[:, nt : nt + 1],
            )
            nc.sync.dma_start(out=out[nt * P : (nt + 1) * P, t0 : t0 + width], in_=res)

        def y_first(nt, t0, width, at):
            y_bank[t0, nt] = bank(at)
            y_mm((t0, nt), 0, 0, nt, t0, width, start=True)

        def y_second(nt, t0, width):
            y_mm((t0, nt), 0, 1, nt, t0, width, stop=True)
            finish((t0, nt), 0, nt, t0, width)

        def y_tile(nt, t0, width, at):
            y_bank[t0, nt] = bank(at)
            cuts = [(0, width)] if width != 3 * CH else [(0, HALF), (HALF, CH)]
            for i, (c0, n) in enumerate(cuts):
                for a in range(2):
                    y_mm((t0, nt), c0, a, nt, t0 + c0, n, start=(i == 0 and a == 0), stop=(i == len(cuts) - 1 and a == 1))
            finish((t0, nt), 0, nt, t0, width)

        def y_short(tiles, t0, at):
            key = (t0, tiles[0])
            y_bank[key] = bank(at)
            for a in range(2):
                for i, nt in enumerate(tiles):
                    y_mm(key, CH * i, a, nt, t0, CH, start=(a == 0 and i == 0), stop=(a == 1 and i == len(tiles) - 1))
            for i, nt in enumerate(tiles):
                finish(key, CH * i, nt, t0, CH)

        def place_bias(at):
            b_t = bank(at)
            nc.tensor.transpose(b_t[:, 0:P], b_rows[:], ident[:])
            nc.scalar.copy(out=bias[:], in_=b_t[:, 0:TILES])

        X, C, WX, WC = ("x", x), ("c", c), ("wx", wx), ("wc", wc)

        load(C, 0, 0, T)
        load(C, 1, 0, T)
        load(WC, 0, 0, R)
        load(WC, 1, 0, R)
        load(WX, 0, 0, R)
        load(X, 0, 0, T)
        load(WX, 1, 0, PASS)
        load(X, 1, 0, HALF)
        load(WX, 1, PASS, R)
        load(X, 1, HALF, T)
        load_w(0, 5)
        load_w(5, TILES)

        for g in range(2):
            round_act("c", g, 0, T, "V", 0, 80)
            round_act("c", g, 0, T, "S", 80, P)
            quant_act("c", g, 0, T)
        round_w("wc", 0, 0, "V", 0, 80)
        round_w("wc", 0, 0, "S", 80, P)
        round_w("wc", 0, 1, "V", 0, 64)
        round_w("wc", 0, 1, "S", 64, P)
        quant_w("wc", 0, 0)
        pc_pass(0, 0)
        quant_w("wc", 0, 1)
        pc_pass(0, 1)
        round_w("wc", 1, 0, "V", 0, 84)
        round_w("wc", 1, 0, "S", 84, P)
        quant_w("wc", 1, 0)
        pc_pass(1, 0)
        round_w("wc", 1, 1, "V", 0, 64)
        round_w("wc", 1, 1, "S", 64, P)
        quant_w("wc", 1, 1)
        pc_pass(1, 1)

        pc_copy(0, 0, "S")
        pc_copy(0, 1, "V")
        pc_copy(0, 2, "S")
        pc_copy(0, 3, "S")
        pc_copy(1, 0, "S")
        pc_copy(1, 1, "S")
        round_w("wx", 0, 0, "V", 0, P)
        round_w("wx", 0, 1, "V", 0, 32)
        round_w("wx", 0, 1, "S", 32, 104)
        quant_w("wx", 0, 0)
        round_act("x", 0, 0, HALF, "V", 0, 64)
        round_act("x", 0, HALF, T, "V", 0, 64)
        place_bias(5)
        quant_act("x", 0, 0, HALF)
        px_pass(0, 0, 0)
        px_pass(0, 0, 1)
        quant_act("x", 0, HALF, T)
        px_pass(0, 0, 2)
        px_pass(0, 0, 3)
        for u in range(2):
            round_w_pair("wx", 1, 0, u, "V", 0, 84)
            round_w_pair("wx", 1, 0, u, "S", 84, P)
        quant_w_pair("wx", 1, 0, 0, 0, 1)
        quant_w_pair("wx", 1, 0, 0, 1, 2)
        round_w("wx", 0, 1, "S", 104, P)
        round_act("x", 1, 0, CH, "V", 0, 32)
        round_act("x", 1, CH, HALF, "S", 0, 32)
        pc_copy(1, 2, "S")
        pc_copy(1, 3, "S")
        quant_w_pair("wx", 1, 0, 1, 0, 1)
        quant_w_pair("wx", 1, 0, 1, 1, 2)
        quant_act("x", 1, 0, CH)
        px_pass(1, 0, 0)
        quant_w("wx", 0, 1)
        quant_act("x", 1, CH, HALF)
        px_pass(1, 0, 1)
        px_pass(0, 1, 0)
        px_pass(0, 1, 1)
        mult(0, 0)
        px_pass(0, 1, 2)
        for u in range(2):
            round_w_pair("wx", 1, 1, u, "V", 0, 84)
            round_w_pair("wx", 1, 1, u, "S", 84, P)
        for j in range(PACK):
            quant_w_pair("wx", 1, 1, j // 2, j % 2, j % 2 + 1)
            px_pass(1, 1, 0, [j])
        px_pass(1, 1, 1)
        px_pass(0, 1, 3)
        round_act("x", 1, HALF, 3 * CH, "S", 0, 32)
        round_act("x", 1, 3 * CH, T, "S", 0, 32)

        mult(0, 1)
        quant_h(0, 0)
        mult(1, 0, 0, 24)
        quant_act("x", 1, HALF, 3 * CH)
        mult(1, 0, 24)
        quant_act("x", 1, 3 * CH, T)
        mult(1, 1)
        quant_h(0, 1)
        quant_h(1, 0)
        quant_h(1, 1)
        px_pass(1, 0, 2)
        px_pass(1, 1, 2)
        px_pass(1, 0, 3)
        px_pass(1, 1, 3)
        y_first(0, 0, HALF, 0)
        y_first(1, 0, HALF, 1)
        y_second(0, 0, HALF)
        y_second(1, 0, HALF)
        y_tile(2, 0, HALF, 4)
        y_tile(3, 0, HALF, 5)
        mult(0, 2)
        mult(1, 2)
        quant_h(0, 2)
        mult(0, 3, 0, 24)
        quant_h(1, 2)
        mult(0, 3, 24)
        mult(1, 3)
        quant_h(0, 3)
        quant_h(1, 3)
        y_tile(4, 0, HALF, 2)
        for nt, at in ((5, 6), (6, 0), (7, 1)):
            y_tile(nt, 0, 3 * CH, at)
        y_first(0, HALF, HALF, 4)
        y_first(1, HALF, HALF, 5)
        y_second(0, HALF, HALF)
        y_second(1, HALF, HALF)
        for nt, at in ((2, 2), (3, 3), (4, 7)):
            y_tile(nt, HALF, HALF, at)
        y_short((5, 6, 7), 3 * CH, 6)
